import numpy as np
import ml_dtypes


def mxq(x, axis, fmt="e4m3"):
    dtype, down = {"e4m3": (ml_dtypes.float8_e4m3fn, 7), "e5m2": (ml_dtypes.float8_e5m2, 14)}[fmt]
    v = np.moveaxis(np.asarray(x, np.float32).astype(ml_dtypes.bfloat16).astype(np.float64), axis, -1)
    blocks = v.reshape(v.shape[:-1] + (-1, 32))
    amax = np.abs(blocks).max(-1, keepdims=True)
    byte = np.maximum(np.where(amax > 0, np.frexp(amax)[1] - 1 + 127, 0) - down, 1)
    scale = np.exp2(byte - 127.0)
    codes = (blocks / scale).astype(np.float32).astype(dtype).astype(np.float64)
    return np.moveaxis((codes * scale).reshape(v.shape), -1, axis)


WIDE = False


def mx_kscale(k):
    if not WIDE:
        return np.ones(k)
    levels = np.array([10, -10, 5, -5, 0])
    if k % 512:
        return np.exp2(np.random.permutation(np.resize(levels, k // 32))).repeat(32)
    a = np.empty((k // 512, 16))
    for p in range(k // 512):
        a[p, :8] = np.random.permutation(np.resize(levels, 8))
        for g in range(8):
            far = levels[np.abs(levels - a[p, g]) >= 10]
            a[p, g + 8] = far[np.random.randint(len(far))]
    return np.exp2(a.ravel()).repeat(32)


def f64(x):
    return np.asarray(x).astype(np.float64)


E2M1 = np.array([0.0, 0.5, 1.0, 1.5, 2.0, 3.0, 4.0, 6.0, -0.0, -0.5, -1.0, -1.5, -2.0, -3.0, -4.0, -6.0])


def pack_weight(w, fmt):
    k, n = w.shape
    w = f64(np.asarray(w, np.float32).astype(ml_dtypes.bfloat16)).reshape(k // 32, 32, n)
    amax = np.abs(w).max(1)
    if fmt == "e4m3":
        byte = np.frexp(amax)[1] - 1 + 127 - 7
    else:
        mant, ex = np.frexp(amax / 6.0)
        byte = np.where(mant > 0.5, ex, ex - 1) + 127
    byte = np.clip(np.where(amax > 0, byte, 1), 1, 254)
    scaled = (w * np.exp2(127.0 - byte)[:, None, :]).reshape(k, n).astype(np.float32)
    by_word = np.ascontiguousarray(scaled.reshape(k // 512, 128, 4, n).transpose(0, 1, 3, 2))
    if fmt == "e4m3":
        words = by_word.astype(ml_dtypes.float8_e4m3fn).view(np.uint8)
    else:
        c = by_word.astype(ml_dtypes.float4_e2m1fn).view(np.uint8) & 0xF
        words = (c[..., 0::2] | (c[..., 1::2] << 4)).reshape(k // 512, 128, 2 * n)
    return np.ascontiguousarray(words), np.ascontiguousarray(byte.astype(np.uint8).reshape(k // 512, 16, n))


def unpack_weight(words, scales, fmt):
    g, _, n = scales.shape
    words = np.ascontiguousarray(words).reshape(g, 128, n, -1)
    if fmt == "e4m3":
        vals = words.view(ml_dtypes.float8_e4m3fn).astype(np.float64)
    else:
        nib = np.empty((g, 128, n, 4), np.uint8)
        nib[..., 0::2] = words & 0xF
        nib[..., 1::2] = words >> 4
        vals = E2M1[nib]
    vals = vals * np.repeat(np.exp2(scales.astype(np.float64) - 127.0), 8, axis=1)[..., None]
    return vals.transpose(0, 1, 3, 2).reshape(g * 512, n)


def gelu(v):
    return 0.5 * v * (1.0 + np.tanh(np.sqrt(2.0 / np.pi) * (v + 0.044715 * v**3)))


O, K, M, T = 512, 1536, 512, 1024


def setup_inputs():
    n = np.random.standard_normal
    s = mx_kscale(K)[:, None]
    x = n((K, T)); x[:O] *= 6.0
    w = n((K, M)) / np.sqrt(K) / s; w[:O] /= 2.0
    p_x4 = pack_weight(x[O:] * s[O:], "e2m1")
    p_w4 = pack_weight(w[O:], "e2m1")
    return {
        "x8": (x[:O] * s[:O]).astype(np.float32),
        "w8": (w[:O]).astype(np.float32),
        "x4_words": p_x4[0],
        "x4_scales": p_x4[1],
        "w4_words": p_w4[0],
        "w4_scales": p_w4[1],
        "b": (0.3 * n(512)).astype(np.float32),
    }


def reference(x8, w8, x4_words, x4_scales, w4_words, w4_scales, b):
    x8_ = mxq(f64(x8), 0, "e4m3")
    w8_ = mxq(f64(w8), 0, "e4m3")
    x4_ = unpack_weight(x4_words, x4_scales, "e2m1")
    w4_ = unpack_weight(w4_words, w4_scales, "e2m1")
    y = w8_.T @ x8_ + w4_.T @ x4_
    return gelu(y + f64(b)[:, None])

@@ -1,0 +1,181 @@
+from contextlib import ExitStack
+
+import concourse.mybir as mybir
+from concourse.masks import make_identity
+
+F32 = mybir.dt.float32
+BF16 = mybir.dt.bfloat16
+I32 = mybir.dt.int32
+U32 = mybir.dt.uint32
+U8 = mybir.dt.uint8
+E4M3 = mybir.dt.float8_e4m3fn_x4
+E2M1 = mybir.dt.float4_e2m1fn_x4
+GELU = mybir.ActivationFunctionType.Gelu_apprx_tanh
+
+P = 128
+K8, K4, N_OUT, T = 512, 1024, 512, 1024
+A = K4 // 512
+MT = N_OUT // P
+TQ = 256
+Q = T // TQ
+SUB = 128
+
+FLOPS = 2 * (K8 + K4) * N_OUT * T
+
+
+def tile_mix_atom_fm_gelu_kernel(tc, x8, w8, x4_words, x4_scales, w4_words, w4_scales, b, out):
+    nc = tc.nc
+    x8_v = x8.rearrange("(p j) t -> p j t", j=4)
+    w8_v = w8.rearrange("(p j) n -> p j n", j=4)
+    x4_v = x4_words.rearrange("a p c -> p a c")
+    w4_v = w4_words.rearrange("a p c -> p a c")
+    out_v = out.rearrange("(m p) t -> p m t", p=P)
+
+    with ExitStack() as ctx:
+        keep = ctx.enter_context(tc.tile_pool(name="keep", bufs=1))
+        stage = ctx.enter_context(tc.tile_pool(name="stage", bufs=1))
+        psum = ctx.enter_context(tc.psum_pool(name="psum", bufs=8))
+        ctx.enter_context(tc.manual_schedule())
+
+        w4 = keep.tile([P, A, 2 * N_OUT], U8, align_bytes=64)
+        x4 = keep.tile([P, A, 2 * T], U8, align_bytes=64)
+        w4s = keep.tile([P, A, N_OUT], U8, align_bytes=64)
+        x4s = keep.tile([P, A, T], U8, align_bytes=64)
+        w8c = keep.tile([P, N_OUT], U32, align_bytes=64)
+        w8s = keep.tile([P, N_OUT], U8, align_bytes=64)
+        x8c = keep.tile([P, T], U32, align_bytes=64)
+        x8s = keep.tile([P, T], U8, align_bytes=64)
+        b_rows = keep.tile([P, P], F32)
+        b_cols = keep.tile([P, MT], F32)
+        ident = keep.tile([P, P], F32)
+        warm = keep.tile([P, 8], F32)
+        warm_out = keep.tile([P, 8], F32)
+
+        def load_w8(h):
+            raw = stage.tile([P, 4, 256], F32, tag="raw_w", bufs=2, name="raw_w")
+            nc.sync.dma_start(out=raw[:], in_=w8_v[:, :, 256 * h : 256 * (h + 1)])
+            return raw
+
+        def load_x8(q):
+            raw = stage.tile([P, 4, TQ], F32, tag="raw_x", bufs=4, name="raw_x")
+            nc.sync.dma_start(out=raw[:], in_=x8_v[:, :, TQ * q : TQ * (q + 1)])
+            return raw
+
+        def regroup(raw, s, engine):
+            grouped = stage.tile([P, SUB, 4], BF16, tag="grouped", bufs=12, align_bytes=64, name="grouped")
+            src = raw[:, :, SUB * s : SUB * (s + 1)].rearrange("p j w -> p w j")
+            if engine == "scalar":
+                nc.scalar.copy(out=grouped[:], in_=src)
+            else:
+                nc.vector.tensor_copy(out=grouped[:], in_=src)
+            return grouped
+
+        def quantise(grouped, codes, scales):
+            nc.vector.quantize_mx(
+                out=codes.bitcast(E4M3),
+                scales=scales,
+                in_=grouped[:].rearrange("p w j -> p (w j)"),
+            )
+
+        nc.gpsimd.memset(w4s[:].rearrange("p a n -> p (a n)").bitcast(I32), 0)
+        nc.vector.memset(x4s[:].rearrange("p a n -> p (a n)").bitcast(I32), 0)
+        nc.vector.memset(warm[:], 0.0)
+        nc.gpsimd.memset(b_rows[:], 0.0)
+        make_identity(nc, ident[:])
+
+        def load_scales(engine, plane, src, r):
+            engine.dma_start(
+                out=plane[32 * r : 32 * r + 4, :, :].bitcast(I32),
+                in_=src[:, 4 * r : 4 * r + 4, :].rearrange("a r n -> r a n").bitcast(I32),
+            )
+
+        raw_w = [None, None]
+        raw_x = [None, None, None, None]
+        nc.sync.dma_start(out=w4[:], in_=w4_v)
+        load_scales(nc.sync, w4s, w4_scales, 0)
+        load_scales(nc.sync, w4s, w4_scales, 1)
+        load_scales(nc.scalar, w4s, w4_scales, 2)
+        load_scales(nc.scalar, w4s, w4_scales, 3)
+        load_scales(nc.scalar, x4s, x4_scales, 0)
+        nc.sync.dma_start(out=x4[:], in_=x4_v)
+        raw_w[0] = load_w8(0)
+        raw_x[0] = load_x8(0)
+        for r in range(1, 4):
+            load_scales(nc.scalar, x4s, x4_scales, r)
+        nc.scalar.dma_start(out=b_rows[0:MT, :], in_=b.rearrange("(m p) -> m p", p=P))
+        nc.scalar.activation(out=warm_out[:], in_=warm[:], func=GELU)
+        raw_w[1] = load_w8(1)
+        for q in range(1, Q):
+            raw_x[q] = load_x8(q)
+
+        acc = {}
+
+        def e2m1_passes(q, ms):
+            for m in ms:
+                bank = psum.tile([P, 512], F32, tag="bank", bufs=8, name="bank")
+                acc[q, m] = bank
+                for a in range(A):
+                    nc.tensor.matmul_mx(
+                        out=bank[:, 0:TQ],
+                        lhsT=w4[:, a, 2 * P * m : 2 * P * (m + 1)].bitcast(E2M1),
+                        lhsT_scale=w4s[:, a, P * m : P * (m + 1)],
+                        rhs=x4[:, a, 2 * TQ * q : 2 * TQ * (q + 1)].bitcast(E2M1),
+                        rhs_scale=x4s[:, a, TQ * q : TQ * (q + 1)],
+                        start=(a == 0),
+                        stop=False,
+                    )
+
+        def e4m3_passes(q, ms):
+            for m in ms:
+                nc.tensor.matmul_mx(
+                    out=acc[q, m][:, 0:TQ],
+                    lhsT=w8c[:, P * m : P * (m + 1)].bitcast(E4M3),
+                    lhsT_scale=w8s[:, P * m : P * (m + 1)],
+                    rhs=x8c[:, TQ * q : TQ * (q + 1)].bitcast(E4M3),
+                    rhs_scale=x8s[:, TQ * q : TQ * (q + 1)],
+                    start=False,
+                    stop=True,
+                )
+
+        def finish(q, ms):
+            o = stage.tile([P, 2, TQ], F32, tag="o", bufs=8, name="o")
+            for i, m in enumerate(ms):
+                nc.scalar.activation(
+                    out=o[:, i, :], in_=acc[q, m][:, 0:TQ], func=GELU, bias=b_cols[:, m : m + 1]
+                )
+            nc.sync.dma_start(
+                out=out_v[:, ms[0] : ms[0] + len(ms), TQ * q : TQ * (q + 1)], in_=o[:, 0 : len(ms), :]
+            )
+
+        def prep_w8(h, engines):
+            g = [regroup(raw_w[h], s, engines[s]) for s in range(2)]
+            for s in range(2):
+                c = slice(256 * h + SUB * s, 256 * h + SUB * (s + 1))
+                quantise(g[s], w8c[:, c], w8s[:, c])
+
+        def prep_x8(q, engines):
+            g = [regroup(raw_x[q], s, engines[s]) for s in range(2)]
+            for s in range(2):
+                c = slice(TQ * q + SUB * s, TQ * q + SUB * (s + 1))
+                quantise(g[s], x8c[:, c], x8s[:, c])
+
+        bias_ps = psum.tile([P, 512], F32, tag="bank", bufs=8, name="bias_ps")
+        prep_w8(0, ("vector", "scalar"))
+        prep_x8(0, ("vector", "vector"))
+        e2m1_passes(0, (0, 1))
+        nc.tensor.transpose(bias_ps[:, 0:P], b_rows[:], ident[:])
+        nc.vector.tensor_copy(out=b_cols[:], in_=bias_ps[:, 0:MT])
+        e4m3_passes(0, (0, 1))
+        finish(0, (0, 1))
+        e2m1_passes(0, (2, 3))
+        e2m1_passes(1, (0, 1))
+        prep_w8(1, ("vector", "vector"))
+        e4m3_passes(0, (2, 3))
+        finish(0, (2, 3))
+        for q in range(1, Q):
+            prep_x8(q, ("vector", "vector"))
+            for ms in ((0, 1), (2, 3)):
+                if (q, ms) != (1, (0, 1)):
+                    e2m1_passes(q, ms)
+                e4m3_passes(q, ms)
+                finish(q, ms)

@@ -1,7 +1,6 @@
 from contextlib import ExitStack
 
 import concourse.mybir as mybir
-from concourse.masks import make_identity
 
 F32 = mybir.dt.float32
 BF16 = mybir.dt.bfloat16
@@ -18,7 +17,6 @@ A = K4 // 512
 MT = N_OUT // P
 TQ = 256
 Q = T // TQ
-SUB = 128
 
 FLOPS = 2 * (K8 + K4) * N_OUT * T
 
@@ -33,41 +31,42 @@ def tile_mix_atom_fm_gelu_kernel(tc, x8, w8, x4_words, x4_scales, w4_words, w4_s
 
     with ExitStack() as ctx:
         keep = ctx.enter_context(tc.tile_pool(name="keep", bufs=1))
-        stage = ctx.enter_context(tc.tile_pool(name="stage", bufs=1))
-        psum = ctx.enter_context(tc.psum_pool(name="psum", bufs=8))
+        psum = ctx.enter_context(tc.psum_pool(name="psum", bufs=1))
         ctx.enter_context(tc.manual_schedule())
 
         w4 = keep.tile([P, A, 2 * N_OUT], U8, align_bytes=64)
-        x4 = keep.tile([P, A, 2 * T], U8, align_bytes=64)
+        x4 = [keep.tile([P, A, T], U8, align_bytes=64, name="x4_%d" % h) for h in range(2)]
         w4s = keep.tile([P, A, N_OUT], U8, align_bytes=64)
         x4s = keep.tile([P, A, T], U8, align_bytes=64)
         w8c = keep.tile([P, N_OUT], U32, align_bytes=64)
         w8s = keep.tile([P, N_OUT], U8, align_bytes=64)
-        x8c = keep.tile([P, T], U32, align_bytes=64)
-        x8s = keep.tile([P, T], U8, align_bytes=64)
-        b_rows = keep.tile([P, P], F32)
-        b_cols = keep.tile([P, MT], F32)
-        ident = keep.tile([P, P], F32)
+        x8c = [keep.tile([P, TQ], U32, align_bytes=64, name="x8c_%d" % q) for q in range(Q)]
+        x8s = [keep.tile([P, TQ], U8, align_bytes=64, name="x8s_%d" % q) for q in range(Q)]
+        raw_w = keep.tile([P, 4, N_OUT], F32)
+        raw_x = [keep.tile([P, 4, TQ], F32, name="raw_x_%d" % q) for q in range(Q)]
+        b_rows = keep.tile([P, P], F32, align_bytes=64)
+        b_cols = keep.tile([P, P], F32, align_bytes=64)
         warm = keep.tile([P, 8], F32)
         warm_out = keep.tile([P, 8], F32)
-
-        def load_w8(h):
-            raw = stage.tile([P, 4, 256], F32, tag="raw_w", bufs=2, name="raw_w")
-            nc.sync.dma_start(out=raw[:], in_=w8_v[:, :, 256 * h : 256 * (h + 1)])
-            return raw
+        banks = {}
+        for q in range(Q):
+            for h in range(2):
+                banks[q, h] = psum.tile([P, 2, TQ], F32, name="bank_%d_%d" % (q, h))
 
         def load_x8(q):
-            raw = stage.tile([P, 4, TQ], F32, tag="raw_x", bufs=4, name="raw_x")
-            nc.sync.dma_start(out=raw[:], in_=x8_v[:, :, TQ * q : TQ * (q + 1)])
-            return raw
+            nc.sync.dma_start(out=raw_x[q][:], in_=x8_v[:, :, TQ * q : TQ * (q + 1)])
 
-        def regroup(raw, s, engine):
-            grouped = stage.tile([P, SUB, 4], BF16, tag="grouped", bufs=12, align_bytes=64, name="grouped")
-            src = raw[:, :, SUB * s : SUB * (s + 1)].rearrange("p j w -> p w j")
+        def load_x4(h):
+            nc.sync.dma_start(out=x4[h][:].bitcast(I32), in_=x4_v[:, :, T * h : T * (h + 1)].bitcast(I32))
+
+        def regroup(raw, c0, width, engine, name):
+            grouped = keep.tile([P, width, 4], BF16, align_bytes=64, name=name)
+            src = raw[:, :, c0 : c0 + width].rearrange("p j (c i) -> p c j i", i=4)
+            dst = grouped[:].rearrange("p (c i) j -> p c j i", i=4)
             if engine == "scalar":
-                nc.scalar.copy(out=grouped[:], in_=src)
+                nc.scalar.copy(out=dst, in_=src)
             else:
-                nc.vector.tensor_copy(out=grouped[:], in_=src)
+                nc.vector.tensor_copy(out=dst, in_=src)
             return grouped
 
         def quantise(grouped, codes, scales):
@@ -77,105 +76,90 @@ def tile_mix_atom_fm_gelu_kernel(tc, x8, w8, x4_words, x4_scales, w4_words, w4_s
                 in_=grouped[:].rearrange("p w j -> p (w j)"),
             )
 
-        nc.gpsimd.memset(w4s[:].rearrange("p a n -> p (a n)").bitcast(I32), 0)
-        nc.vector.memset(x4s[:].rearrange("p a n -> p (a n)").bitcast(I32), 0)
-        nc.vector.memset(warm[:], 0.0)
-        nc.gpsimd.memset(b_rows[:], 0.0)
-        make_identity(nc, ident[:])
+        def load_scales(plane, src):
+            for r in range(4):
+                nc.sync.dma_start(
+                    out=plane[32 * r : 32 * r + 4, :, :].bitcast(I32),
+                    in_=src[:, 4 * r : 4 * r + 4, :].rearrange("a r n -> r a n").bitcast(I32),
+                )
 
-        def load_scales(engine, plane, src, r):
-            engine.dma_start(
-                out=plane[32 * r : 32 * r + 4, :, :].bitcast(I32),
-                in_=src[:, 4 * r : 4 * r + 4, :].rearrange("a r n -> r a n").bitcast(I32),
+        def load_w8(h):
+            nc.sync.dma_start(
+                out=raw_w[:, 2 * h : 2 * h + 2, :].rearrange("p j n -> p (j n)"),
+                in_=w8_v[:, 2 * h : 2 * h + 2, :].rearrange("p j n -> p (j n)"),
             )
 
-        raw_w = [None, None]
-        raw_x = [None, None, None, None]
-        nc.sync.dma_start(out=w4[:], in_=w4_v)
-        load_scales(nc.sync, w4s, w4_scales, 0)
-        load_scales(nc.sync, w4s, w4_scales, 1)
-        load_scales(nc.scalar, w4s, w4_scales, 2)
-        load_scales(nc.scalar, w4s, w4_scales, 3)
-        load_scales(nc.scalar, x4s, x4_scales, 0)
-        nc.sync.dma_start(out=x4[:], in_=x4_v)
-        raw_w[0] = load_w8(0)
-        raw_x[0] = load_x8(0)
-        for r in range(1, 4):
-            load_scales(nc.scalar, x4s, x4_scales, r)
-        nc.scalar.dma_start(out=b_rows[0:MT, :], in_=b.rearrange("(m p) -> m p", p=P))
+        nc.vector.memset(w4s[:].rearrange("p a n -> p (a n)").bitcast(I32), 0)
+        nc.vector.memset(b_rows[:], 0.0)
+        nc.vector.memset(x4s[:].rearrange("p a n -> p (a n)").bitcast(I32), 0)
+        nc.vector.memset(warm[:], 0.0)
         nc.scalar.activation(out=warm_out[:], in_=warm[:], func=GELU)
-        raw_w[1] = load_w8(1)
+
+        load_w8(0)
+        load_scales(w4s, w4_scales)
+        load_w8(1)
+        nc.sync.dma_start(out=w4[:].bitcast(I32), in_=w4_v.bitcast(I32))
+        nc.sync.dma_start(
+            out=b_rows[0:P:32, :].rearrange("q (m i) -> q m i", i=32),
+            in_=b.rearrange("(m q i) -> q m i", q=4, i=32),
+        )
+        load_scales(x4s, x4_scales)
+        load_x4(0)
+        load_x8(0)
+        load_x4(1)
         for q in range(1, Q):
-            raw_x[q] = load_x8(q)
+            load_x8(q)
 
-        acc = {}
-
-        def e2m1_passes(q, ms):
-            for m in ms:
-                bank = psum.tile([P, 512], F32, tag="bank", bufs=8, name="bank")
-                acc[q, m] = bank
+        def e2m1_passes(q):
+            half, c0 = divmod(TQ * q, T // 2)
+            for m in range(MT):
                 for a in range(A):
                     nc.tensor.matmul_mx(
-                        out=bank[:, 0:TQ],
+                        out=banks[q, m // 2][:, m % 2, :],
                         lhsT=w4[:, a, 2 * P * m : 2 * P * (m + 1)].bitcast(E2M1),
                         lhsT_scale=w4s[:, a, P * m : P * (m + 1)],
-                        rhs=x4[:, a, 2 * TQ * q : 2 * TQ * (q + 1)].bitcast(E2M1),
+                        rhs=x4[half][:, a, 2 * c0 : 2 * (c0 + TQ)].bitcast(E2M1),
                         rhs_scale=x4s[:, a, TQ * q : TQ * (q + 1)],
-                        start=(a == 0),
+                        start=(a == 0 and m % 2 == 0),
                         stop=False,
                     )
 
-        def e4m3_passes(q, ms):
-            for m in ms:
+        def e4m3_passes(q):
+            for m in range(MT):
                 nc.tensor.matmul_mx(
-                    out=acc[q, m][:, 0:TQ],
+                    out=banks[q, m // 2][:, m % 2, :],
                     lhsT=w8c[:, P * m : P * (m + 1)].bitcast(E4M3),
                     lhsT_scale=w8s[:, P * m : P * (m + 1)],
-                    rhs=x8c[:, TQ * q : TQ * (q + 1)].bitcast(E4M3),
-                    rhs_scale=x8s[:, TQ * q : TQ * (q + 1)],
+                    rhs=x8c[q][:].bitcast(E4M3),
+                    rhs_scale=x8s[q][:],
                     start=False,
-                    stop=True,
+                    stop=(m % 2 == 1),
                 )
 
-        def finish(q, ms):
-            o = stage.tile([P, 2, TQ], F32, tag="o", bufs=8, name="o")
-            for i, m in enumerate(ms):
-                nc.scalar.activation(
-                    out=o[:, i, :], in_=acc[q, m][:, 0:TQ], func=GELU, bias=b_cols[:, m : m + 1]
-                )
-            nc.sync.dma_start(
-                out=out_v[:, ms[0] : ms[0] + len(ms), TQ * q : TQ * (q + 1)], in_=o[:, 0 : len(ms), :]
-            )
+        def finish(q):
+            for h in range(2):
+                o = keep.tile([P, 2, TQ], F32, name="o_%d_%d" % (q, h))
+                for i in range(2):
+                    m = 2 * h + i
+                    nc.scalar.activation(
+                        out=o[:, i, :], in_=banks[q, h][:, i, :], func=GELU, bias=b_cols[:, 32 * m : 32 * m + 1]
+                    )
+                nc.sync.dma_start(out=out_v[:, 2 * h : 2 * h + 2, TQ * q : TQ * (q + 1)], in_=o[:])
 
-        def prep_w8(h, engines):
-            g = [regroup(raw_w[h], s, engines[s]) for s in range(2)]
+        def prep_x8(q):
+            g = [regroup(raw_x[q], P * s, P, "vector", "gx_%d_%d" % (q, s)) for s in range(2)]
             for s in range(2):
-                c = slice(256 * h + SUB * s, 256 * h + SUB * (s + 1))
-                quantise(g[s], w8c[:, c], w8s[:, c])
+                quantise(g[s], x8c[q][:, P * s : P * (s + 1)], x8s[q][:, P * s : P * (s + 1)])
 
-        def prep_x8(q, engines):
-            g = [regroup(raw_x[q], s, engines[s]) for s in range(2)]
-            for s in range(2):
-                c = slice(TQ * q + SUB * s, TQ * q + SUB * (s + 1))
-                quantise(g[s], x8c[:, c], x8s[:, c])
-
-        bias_ps = psum.tile([P, 512], F32, tag="bank", bufs=8, name="bias_ps")
-        prep_w8(0, ("vector", "scalar"))
-        prep_x8(0, ("vector", "vector"))
-        e2m1_passes(0, (0, 1))
-        nc.tensor.transpose(bias_ps[:, 0:P], b_rows[:], ident[:])
-        nc.vector.tensor_copy(out=b_cols[:], in_=bias_ps[:, 0:MT])
-        e4m3_passes(0, (0, 1))
-        finish(0, (0, 1))
-        e2m1_passes(0, (2, 3))
-        e2m1_passes(1, (0, 1))
-        prep_w8(1, ("vector", "vector"))
-        e4m3_passes(0, (2, 3))
-        finish(0, (2, 3))
-        for q in range(1, Q):
-            prep_x8(q, ("vector", "vector"))
-            for ms in ((0, 1), (2, 3)):
-                if (q, ms) != (1, (0, 1)):
-                    e2m1_passes(q, ms)
-                e4m3_passes(q, ms)
-                finish(q, ms)
+        e2m1_passes(0)
+        e2m1_passes(1)
+        gw = [regroup(raw_w, P * m, P, "scalar" if m == 3 else "vector", "gw_%d" % m) for m in range(MT)]
+        nc.vector.transpose(out=b_cols[:], in_=b_rows[:])
+        for m in range(MT):
+            quantise(gw[m], w8c[:, P * m : P * (m + 1)], w8s[:, P * m : P * (m + 1)])
+        for q in range(Q):
+            prep_x8(q)
+            e4m3_passes(q)
+            finish(q)
+            if q + 2 < Q:
+                e2m1_passes(q + 2)

@@ -15,8 +15,8 @@ P = 128
 K8, K4, N_OUT, T = 512, 1024, 512, 1024
 A = K4 // 512
 MT = N_OUT // P
+TH = T // 2
 TQ = 256
-Q = T // TQ
 
 FLOPS = 2 * (K8 + K4) * N_OUT * T
 
@@ -40,41 +40,23 @@ def tile_mix_atom_fm_gelu_kernel(tc, x8, w8, x4_words, x4_scales, w4_words, w4_s
         x4s = keep.tile([P, A, T], U8, align_bytes=64)
         w8c = keep.tile([P, N_OUT], U32, align_bytes=64)
         w8s = keep.tile([P, N_OUT], U8, align_bytes=64)
-        x8c = [keep.tile([P, TQ], U32, align_bytes=64, name="x8c_%d" % q) for q in range(Q)]
-        x8s = [keep.tile([P, TQ], U8, align_bytes=64, name="x8s_%d" % q) for q in range(Q)]
+        x8c = [keep.tile([P, TH], U32, align_bytes=64, name="x8c_%d" % h) for h in range(2)]
+        x8s = [keep.tile([P, TH], U8, align_bytes=64, name="x8s_%d" % h) for h in range(2)]
         raw_w = keep.tile([P, 4, N_OUT], F32)
-        raw_x = [keep.tile([P, 4, TQ], F32, name="raw_x_%d" % q) for q in range(Q)]
+        raw_first = keep.tile([P, 4, TH], F32)
+        raw_last = [keep.tile([P, 4, TQ], F32, name="raw_last_%d" % s) for s in range(2)]
+        res = [keep.tile([P, MT, TH], F32, name="res_%d" % h) for h in range(2)]
         b_rows = keep.tile([P, P], F32, align_bytes=64)
         b_cols = keep.tile([P, P], F32, align_bytes=64)
         warm = keep.tile([P, 8], F32)
         warm_out = keep.tile([P, 8], F32)
-        banks = {}
-        for q in range(Q):
-            for h in range(2):
-                banks[q, h] = psum.tile([P, 2, TQ], F32, name="bank_%d_%d" % (q, h))
+        banks = [[psum.tile([P, 2, TQ], F32, name="bank_%d_%d" % (q, g)) for g in range(2)] for q in range(4)]
 
-        def load_x8(q):
-            nc.sync.dma_start(out=raw_x[q][:], in_=x8_v[:, :, TQ * q : TQ * (q + 1)])
+        def load_x8(raw, t0, width):
+            nc.sync.dma_start(out=raw[:], in_=x8_v[:, :, t0 : t0 + width])
 
         def load_x4(h):
             nc.sync.dma_start(out=x4[h][:].bitcast(I32), in_=x4_v[:, :, T * h : T * (h + 1)].bitcast(I32))
-
-        def regroup(raw, c0, width, engine, name):
-            grouped = keep.tile([P, width, 4], BF16, align_bytes=64, name=name)
-            src = raw[:, :, c0 : c0 + width].rearrange("p j (c i) -> p c j i", i=4)
-            dst = grouped[:].rearrange("p (c i) j -> p c j i", i=4)
-            if engine == "scalar":
-                nc.scalar.copy(out=dst, in_=src)
-            else:
-                nc.vector.tensor_copy(out=dst, in_=src)
-            return grouped
-
-        def quantise(grouped, codes, scales):
-            nc.vector.quantize_mx(
-                out=codes.bitcast(E4M3),
-                scales=scales,
-                in_=grouped[:].rearrange("p w j -> p (w j)"),
-            )
 
         def load_scales(plane, src):
             for r in range(4):
@@ -83,83 +65,131 @@ def tile_mix_atom_fm_gelu_kernel(tc, x8, w8, x4_words, x4_scales, w4_words, w4_s
                     in_=src[:, 4 * r : 4 * r + 4, :].rearrange("a r n -> r a n").bitcast(I32),
                 )
 
-        def load_w8(h):
+        def load_w8():
+            nc.sync.dma_start(out=raw_w[:].rearrange("p j n -> p (j n)"), in_=w8_v.rearrange("p j n -> p (j n)"))
+
+        def load_bias():
             nc.sync.dma_start(
-                out=raw_w[:, 2 * h : 2 * h + 2, :].rearrange("p j n -> p (j n)"),
-                in_=w8_v[:, 2 * h : 2 * h + 2, :].rearrange("p j n -> p (j n)"),
+                out=b_rows[0:P:32, :].rearrange("q (m i) -> q m i", i=32),
+                in_=b.rearrange("(m q i) -> q m i", q=4, i=32),
+            )
+
+        def regroup(raw, s, engine, name):
+            grouped = keep.tile([P, P, 4], BF16, align_bytes=64, name=name)
+            src = raw[:, :, P * s : P * (s + 1)].rearrange("p j (c i) -> p c j i", i=4)
+            dst = grouped[:].rearrange("p (c i) j -> p c j i", i=4)
+            if engine == "scalar":
+                nc.scalar.copy(out=dst, in_=src)
+            else:
+                nc.vector.tensor_copy(out=dst, in_=src)
+            return grouped
+
+        def quantise(grouped, codes, scales, s):
+            nc.vector.quantize_mx(
+                out=codes[:, P * s : P * (s + 1)].bitcast(E4M3),
+                scales=scales[:, P * s : P * (s + 1)],
+                in_=grouped[:].rearrange("p w j -> p (w j)"),
+            )
+
+        def e2m1_pass(acc, m, a, t0, width, start):
+            h, c0 = divmod(t0, TH)
+            nc.tensor.matmul_mx(
+                out=acc,
+                lhsT=w4[:, a, 2 * P * m : 2 * P * (m + 1)].bitcast(E2M1),
+                lhsT_scale=w4s[:, a, P * m : P * (m + 1)],
+                rhs=x4[h][:, a, 2 * c0 : 2 * (c0 + width)].bitcast(E2M1),
+                rhs_scale=x4s[:, a, t0 : t0 + width],
+                start=start,
+                stop=False,
+            )
+
+        def e4m3_pass(acc, m, t0, width, stop):
+            h, c0 = divmod(t0, TH)
+            nc.tensor.matmul_mx(
+                out=acc,
+                lhsT=w8c[:, P * m : P * (m + 1)].bitcast(E4M3),
+                lhsT_scale=w8s[:, P * m : P * (m + 1)],
+                rhs=x8c[h][:, c0 : c0 + width].bitcast(E4M3),
+                rhs_scale=x8s[h][:, c0 : c0 + width],
+                start=False,
+                stop=stop,
+            )
+
+        def gelu(dst, acc, m):
+            nc.scalar.activation(out=dst, in_=acc, func=GELU, bias=b_cols[:, 32 * m : 32 * m + 1])
+
+        def store(m0, count, t0, width):
+            h, c0 = divmod(t0, TH)
+            nc.sync.dma_start(
+                out=out_v[:, m0 : m0 + count, t0 : t0 + width], in_=res[h][:, m0 : m0 + count, c0 : c0 + width]
             )
 
         nc.vector.memset(w4s[:].rearrange("p a n -> p (a n)").bitcast(I32), 0)
-        nc.vector.memset(b_rows[:], 0.0)
         nc.vector.memset(x4s[:].rearrange("p a n -> p (a n)").bitcast(I32), 0)
         nc.vector.memset(warm[:], 0.0)
+        nc.vector.memset(b_rows[:], 0.0)
         nc.scalar.activation(out=warm_out[:], in_=warm[:], func=GELU)
 
-        load_w8(0)
-        load_scales(w4s, w4_scales)
-        load_w8(1)
         nc.sync.dma_start(out=w4[:].bitcast(I32), in_=w4_v.bitcast(I32))
-        nc.sync.dma_start(
-            out=b_rows[0:P:32, :].rearrange("q (m i) -> q m i", i=32),
-            in_=b.rearrange("(m q i) -> q m i", q=4, i=32),
-        )
-        load_scales(x4s, x4_scales)
         load_x4(0)
-        load_x8(0)
+        load_scales(w4s, w4_scales)
+        load_w8()
+        load_scales(x4s, x4_scales)
+        load_bias()
+        load_x8(raw_first, 0, TH)
         load_x4(1)
-        for q in range(1, Q):
-            load_x8(q)
+        for s in range(2):
+            load_x8(raw_last[s], TH + TQ * s, TQ)
 
-        def e2m1_passes(q):
-            half, c0 = divmod(TQ * q, T // 2)
-            for m in range(MT):
+        for i in range(3):
+            nc.tensor.matmul_mx(
+                out=banks[3][1][:].rearrange("p i t -> p (i t)"),
+                lhsT=w4[:, 0, 0 : 2 * P].bitcast(E2M1),
+                lhsT_scale=w4s[:, 0, 0:P],
+                rhs=w4[:, 1, :].bitcast(E2M1),
+                rhs_scale=w4s[:, 1, :],
+                start=True,
+                stop=True,
+            )
+
+        def open_bank(q, g):
+            for i in range(2):
                 for a in range(A):
-                    nc.tensor.matmul_mx(
-                        out=banks[q, m // 2][:, m % 2, :],
-                        lhsT=w4[:, a, 2 * P * m : 2 * P * (m + 1)].bitcast(E2M1),
-                        lhsT_scale=w4s[:, a, P * m : P * (m + 1)],
-                        rhs=x4[half][:, a, 2 * c0 : 2 * (c0 + TQ)].bitcast(E2M1),
-                        rhs_scale=x4s[:, a, TQ * q : TQ * (q + 1)],
-                        start=(a == 0 and m % 2 == 0),
-                        stop=False,
-                    )
+                    e2m1_pass(banks[q][g][:, i, :], 2 * g + i, a, TQ * q, TQ, a == 0 and i == 0)
 
-        def e4m3_passes(q):
-            for m in range(MT):
-                nc.tensor.matmul_mx(
-                    out=banks[q, m // 2][:, m % 2, :],
-                    lhsT=w8c[:, P * m : P * (m + 1)].bitcast(E4M3),
-                    lhsT_scale=w8s[:, P * m : P * (m + 1)],
-                    rhs=x8c[q][:].bitcast(E4M3),
-                    rhs_scale=x8s[q][:],
-                    start=False,
-                    stop=(m % 2 == 1),
-                )
+        def close_bank(q, g):
+            h, s = divmod(q, 2)
+            for i in range(2):
+                e4m3_pass(banks[q][g][:, i, :], 2 * g + i, TQ * q, TQ, i == 1)
+            for i in range(2):
+                m = 2 * g + i
+                gelu(res[h][:, m, TQ * s : TQ * (s + 1)], banks[q][g][:, i, :], m)
+            store(2 * g, 2, TQ * q, TQ)
 
-        def finish(q):
-            for h in range(2):
-                o = keep.tile([P, 2, TQ], F32, name="o_%d_%d" % (q, h))
-                for i in range(2):
-                    m = 2 * h + i
-                    nc.scalar.activation(
-                        out=o[:, i, :], in_=banks[q, h][:, i, :], func=GELU, bias=b_cols[:, 32 * m : 32 * m + 1]
-                    )
-                nc.sync.dma_start(out=out_v[:, 2 * h : 2 * h + 2, TQ * q : TQ * (q + 1)], in_=o[:])
+        for q in range(2):
+            for g in range(2):
+                open_bank(q, g)
 
-        def prep_x8(q):
-            g = [regroup(raw_x[q], P * s, P, "vector", "gx_%d_%d" % (q, s)) for s in range(2)]
-            for s in range(2):
-                quantise(g[s], x8c[q][:, P * s : P * (s + 1)], x8s[q][:, P * s : P * (s + 1)])
-
-        e2m1_passes(0)
-        e2m1_passes(1)
-        gw = [regroup(raw_w, P * m, P, "scalar" if m == 3 else "vector", "gw_%d" % m) for m in range(MT)]
+        gw = [regroup(raw_w, s, "scalar" if s == 3 else "vector", "gw_%d" % s) for s in range(4)]
+        for s in range(4):
+            quantise(gw[s], w8c, w8s, s)
         nc.vector.transpose(out=b_cols[:], in_=b_rows[:])
-        for m in range(MT):
-            quantise(gw[m], w8c[:, P * m : P * (m + 1)], w8s[:, P * m : P * (m + 1)])
-        for q in range(Q):
-            prep_x8(q)
-            e4m3_passes(q)
-            finish(q)
-            if q + 2 < Q:
-                e2m1_passes(q + 2)
+
+        opens_after = (((2, 0),), ((2, 1), (3, 0)), ((3, 1),), ())
+        early = regroup(raw_first, 2, "scalar", "gx_early")
+        for q in range(4):
+            h, s = divmod(q, 2)
+            gx = []
+            for i in range(2):
+                if (q, i) == (1, 0):
+                    gx.append(early)
+                elif h == 0:
+                    gx.append(regroup(raw_first, 2 * s + i, "vector", "gx_%d_%d" % (q, i)))
+                else:
+                    gx.append(regroup(raw_last[s], i, "vector", "gx_%d_%d" % (q, i)))
+            for i in range(2):
+                quantise(gx[i], x8c[h], x8s[h], 2 * s + i)
+            for g in range(2):
+                close_bank(q, g)
+            for later in opens_after[q]:
+                open_bank(*later)

@@ -43,8 +43,7 @@ def tile_mix_atom_fm_gelu_kernel(tc, x8, w8, x4_words, x4_scales, w4_words, w4_s
         x8c = [keep.tile([P, TH], U32, align_bytes=64, name="x8c_%d" % h) for h in range(2)]
         x8s = [keep.tile([P, TH], U8, align_bytes=64, name="x8s_%d" % h) for h in range(2)]
         raw_w = keep.tile([P, 4, N_OUT], F32)
-        raw_first = keep.tile([P, 4, TH], F32)
-        raw_last = [keep.tile([P, 4, TQ], F32, name="raw_last_%d" % s) for s in range(2)]
+        raw_x = [keep.tile([P, 4, TQ], F32, name="raw_x_%d" % q) for q in range(4)]
         res = [keep.tile([P, MT, TH], F32, name="res_%d" % h) for h in range(2)]
         b_rows = keep.tile([P, P], F32, align_bytes=64)
         b_cols = keep.tile([P, P], F32, align_bytes=64)
@@ -52,8 +51,8 @@ def tile_mix_atom_fm_gelu_kernel(tc, x8, w8, x4_words, x4_scales, w4_words, w4_s
         warm_out = keep.tile([P, 8], F32)
         banks = [[psum.tile([P, 2, TQ], F32, name="bank_%d_%d" % (q, g)) for g in range(2)] for q in range(4)]
 
-        def load_x8(raw, t0, width):
-            nc.sync.dma_start(out=raw[:], in_=x8_v[:, :, t0 : t0 + width])
+        def load_x8(q):
+            nc.sync.dma_start(out=raw_x[q][:], in_=x8_v[:, :, TQ * q : TQ * (q + 1)])
 
         def load_x4(h):
             nc.sync.dma_start(out=x4[h][:].bitcast(I32), in_=x4_v[:, :, T * h : T * (h + 1)].bitcast(I32))
@@ -61,8 +60,8 @@ def tile_mix_atom_fm_gelu_kernel(tc, x8, w8, x4_words, x4_scales, w4_words, w4_s
         def load_scales(plane, src):
             for r in range(4):
                 nc.sync.dma_start(
-                    out=plane[32 * r : 32 * r + 4, :, :].bitcast(I32),
-                    in_=src[:, 4 * r : 4 * r + 4, :].rearrange("a r n -> r a n").bitcast(I32),
+                    out=plane[r:P:32, :, :].bitcast(I32),
+                    in_=src.rearrange("a (q r) n -> r q a n", r=4)[r].bitcast(I32),
                 )
 
         def load_w8():
@@ -136,10 +135,11 @@ def tile_mix_atom_fm_gelu_kernel(tc, x8, w8, x4_words, x4_scales, w4_words, w4_s
         load_w8()
         load_scales(x4s, x4_scales)
         load_bias()
-        load_x8(raw_first, 0, TH)
+        load_x8(0)
+        load_x8(1)
         load_x4(1)
-        for s in range(2):
-            load_x8(raw_last[s], TH + TQ * s, TQ)
+        load_x8(2)
+        load_x8(3)
 
         for i in range(3):
             nc.tensor.matmul_mx(
@@ -166,29 +166,30 @@ def tile_mix_atom_fm_gelu_kernel(tc, x8, w8, x4_words, x4_scales, w4_words, w4_s
                 gelu(res[h][:, m, TQ * s : TQ * (s + 1)], banks[q][g][:, i, :], m)
             store(2 * g, 2, TQ * q, TQ)
 
-        for q in range(2):
-            for g in range(2):
-                open_bank(q, g)
+        def regroup_x8(q):
+            return [regroup(raw_x[q], i, "vector", "gx_%d_%d" % (q, i)) for i in range(2)]
 
-        gw = [regroup(raw_w, s, "scalar" if s == 3 else "vector", "gw_%d" % s) for s in range(4)]
-        for s in range(4):
-            quantise(gw[s], w8c, w8s, s)
-        nc.vector.transpose(out=b_cols[:], in_=b_rows[:])
-
-        opens_after = (((2, 0),), ((2, 1), (3, 0)), ((3, 1),), ())
-        early = regroup(raw_first, 2, "scalar", "gx_early")
-        for q in range(4):
+        def quantise_x8(q, gx):
             h, s = divmod(q, 2)
-            gx = []
-            for i in range(2):
-                if (q, i) == (1, 0):
-                    gx.append(early)
-                elif h == 0:
-                    gx.append(regroup(raw_first, 2 * s + i, "vector", "gx_%d_%d" % (q, i)))
-                else:
-                    gx.append(regroup(raw_last[s], i, "vector", "gx_%d_%d" % (q, i)))
             for i in range(2):
                 quantise(gx[i], x8c[h], x8s[h], 2 * s + i)
+
+        gw = [regroup(raw_w, m, "vector" if m < 2 else "scalar", "gw_%d" % m) for m in range(MT)]
+        quantise(gw[0], w8c, w8s, 0)
+        quantise(gw[1], w8c, w8s, 1)
+        gx = regroup_x8(0)
+        nc.vector.transpose(out=b_cols[:], in_=b_rows[:])
+        quantise_x8(0, gx)
+        quantise(gw[2], w8c, w8s, 2)
+        quantise(gw[3], w8c, w8s, 3)
+
+        open_bank(0, 0)
+        open_bank(0, 1)
+        open_bank(1, 0)
+        opens_after = (((1, 1), (2, 0)), ((2, 1), (3, 0)), ((3, 1),), ())
+        for q in range(4):
+            if q > 0:
+                quantise_x8(q, regroup_x8(q))
             for g in range(2):
                 close_bank(q, g)
             for later in opens_after[q]:

@@ -75,8 +75,8 @@ def tile_mix_atom_fm_gelu_kernel(tc, x8, w8, x4_words, x4_scales, w4_words, w4_s
 
         def regroup(raw, s, engine, name):
             grouped = keep.tile([P, P, 4], BF16, align_bytes=64, name=name)
-            src = raw[:, :, P * s : P * (s + 1)].rearrange("p j (c i) -> p c j i", i=4)
-            dst = grouped[:].rearrange("p (c i) j -> p c j i", i=4)
+            src = raw[:, :, P * s : P * (s + 1)].rearrange("p j (c i) -> p c j i", i=2)
+            dst = grouped[:].rearrange("p (c i) j -> p c j i", i=2)
             if engine == "scalar":
                 nc.scalar.copy(out=dst, in_=src)
             else:

@@ -13,18 +13,24 @@ GELU = mybir.ActivationFunctionType.Gelu_apprx_tanh
 
 P = 128
 K8, K4, N_OUT, T = 512, 1024, 512, 1024
-A = K4 // 512
-MT = N_OUT // P
-TH = T // 2
-TQ = 256
+PACK = 4
+QUAD = 32
+PASSES4 = K4 // (P * PACK)
+BLOCKS = N_OUT // P
+HALF = T // 2
+QUARTER = T // 4
+PAIR = 2
+W8_AHEAD = 3
+WARM_PASSES = 3
+OPENS_BEFORE = (4, 0, 1, 0, 1, 0, 1, 1)
 
 FLOPS = 2 * (K8 + K4) * N_OUT * T
 
 
 def tile_mix_atom_fm_gelu_kernel(tc, x8, w8, x4_words, x4_scales, w4_words, w4_scales, b, out):
     nc = tc.nc
-    x8_v = x8.rearrange("(p j) t -> p j t", j=4)
-    w8_v = w8.rearrange("(p j) n -> p j n", j=4)
+    x8_v = x8.rearrange("(p j) t -> p j t", j=PACK)
+    w8_v = w8.rearrange("(p j) n -> p j n", j=PACK)
     x4_v = x4_words.rearrange("a p c -> p a c")
     w4_v = w4_words.rearrange("a p c -> p a c")
     out_v = out.rearrange("(m p) t -> p m t", p=P)
@@ -34,53 +40,58 @@ def tile_mix_atom_fm_gelu_kernel(tc, x8, w8, x4_words, x4_scales, w4_words, w4_s
         psum = ctx.enter_context(tc.psum_pool(name="psum", bufs=1))
         ctx.enter_context(tc.manual_schedule())
 
-        w4 = keep.tile([P, A, 2 * N_OUT], U8, align_bytes=64)
-        x4 = [keep.tile([P, A, T], U8, align_bytes=64, name="x4_%d" % h) for h in range(2)]
-        w4s = keep.tile([P, A, N_OUT], U8, align_bytes=64)
-        x4s = keep.tile([P, A, T], U8, align_bytes=64)
+        w4 = keep.tile([P, PASSES4, 2 * N_OUT], U8, align_bytes=64)
+        x4 = [keep.tile([P, PASSES4, 2 * HALF], U8, align_bytes=64, name="x4_%d" % h) for h in range(2)]
+        w4s = keep.tile([P, PASSES4, N_OUT], U8, align_bytes=64)
+        x4s = keep.tile([P, PASSES4, T], U8, align_bytes=64)
         w8c = keep.tile([P, N_OUT], U32, align_bytes=64)
         w8s = keep.tile([P, N_OUT], U8, align_bytes=64)
-        x8c = [keep.tile([P, TH], U32, align_bytes=64, name="x8c_%d" % h) for h in range(2)]
-        x8s = [keep.tile([P, TH], U8, align_bytes=64, name="x8s_%d" % h) for h in range(2)]
-        raw_w = keep.tile([P, 4, N_OUT], F32)
-        raw_x = [keep.tile([P, 4, TQ], F32, name="raw_x_%d" % q) for q in range(4)]
-        res = [keep.tile([P, MT, TH], F32, name="res_%d" % h) for h in range(2)]
+        x8c = [keep.tile([P, HALF], U32, align_bytes=64, name="x8c_%d" % h) for h in range(2)]
+        x8s = [keep.tile([P, HALF], U8, align_bytes=64, name="x8s_%d" % h) for h in range(2)]
+        raw_w = keep.tile([P, PACK, N_OUT], F32)
+        raw_x = [keep.tile([P, PACK, QUARTER], F32, name="raw_x_%d" % q) for q in range(4)]
+        res = [keep.tile([P, BLOCKS, HALF], F32, name="res_%d" % h) for h in range(2)]
         b_rows = keep.tile([P, P], F32, align_bytes=64)
         b_cols = keep.tile([P, P], F32, align_bytes=64)
         warm = keep.tile([P, 8], F32)
         warm_out = keep.tile([P, 8], F32)
-        banks = [[psum.tile([P, 2, TQ], F32, name="bank_%d_%d" % (q, g)) for g in range(2)] for q in range(4)]
+        banks = [
+            [psum.tile([P, PAIR, QUARTER], F32, name="bank_%d_%d" % (q, g)) for g in range(PAIR)] for q in range(4)
+        ]
 
         def load_x8(q):
-            nc.sync.dma_start(out=raw_x[q][:], in_=x8_v[:, :, TQ * q : TQ * (q + 1)])
+            nc.sync.dma_start(out=raw_x[q][:], in_=x8_v[:, :, QUARTER * q : QUARTER * (q + 1)])
 
         def load_x4(h):
-            nc.sync.dma_start(out=x4[h][:].bitcast(I32), in_=x4_v[:, :, T * h : T * (h + 1)].bitcast(I32))
+            nc.sync.dma_start(
+                out=x4[h][:].bitcast(I32), in_=x4_v[:, :, 2 * HALF * h : 2 * HALF * (h + 1)].bitcast(I32)
+            )
 
         def load_scales(plane, src):
             for r in range(4):
                 nc.sync.dma_start(
-                    out=plane[r:P:32, :, :].bitcast(I32),
-                    in_=src.rearrange("a (q r) n -> r q a n", r=4)[r].bitcast(I32),
+                    out=plane[r:P:QUAD, :, :].bitcast(I32),
+                    in_=src.rearrange("a (v r) n -> r v a n", r=4)[r].bitcast(I32),
                 )
 
-        def load_w8():
-            nc.sync.dma_start(out=raw_w[:].rearrange("p j n -> p (j n)"), in_=w8_v.rearrange("p j n -> p (j n)"))
+        def load_w8(j0, j1):
+            nc.sync.dma_start(
+                out=raw_w[:, j0:j1, :].rearrange("p j n -> p (j n)"),
+                in_=w8_v[:, j0:j1, :].rearrange("p j n -> p (j n)"),
+            )
 
         def load_bias():
             nc.sync.dma_start(
-                out=b_rows[0:P:32, :].rearrange("q (m i) -> q m i", i=32),
-                in_=b.rearrange("(m q i) -> q m i", q=4, i=32),
+                out=b_rows[0:P:QUAD, :].rearrange("v (m i) -> v m i", i=QUAD),
+                in_=b.rearrange("(m v i) -> v m i", v=4, i=QUAD),
             )
 
-        def regroup(raw, s, engine, name):
-            grouped = keep.tile([P, P, 4], BF16, align_bytes=64, name=name)
-            src = raw[:, :, P * s : P * (s + 1)].rearrange("p j (c i) -> p c j i", i=2)
-            dst = grouped[:].rearrange("p (c i) j -> p c j i", i=2)
-            if engine == "scalar":
-                nc.scalar.copy(out=dst, in_=src)
-            else:
-                nc.vector.tensor_copy(out=dst, in_=src)
+        def regroup(raw, s, copy, name):
+            grouped = keep.tile([P, P, PACK], BF16, align_bytes=64, name=name)
+            copy(
+                out=grouped[:].rearrange("p (c i) j -> p c j i", i=2),
+                in_=raw[:, :, P * s : P * (s + 1)].rearrange("p j (c i) -> p c j i", i=2),
+            )
             return grouped
 
         def quantise(grouped, codes, scales, s):
@@ -90,50 +101,66 @@ def tile_mix_atom_fm_gelu_kernel(tc, x8, w8, x4_words, x4_scales, w4_words, w4_s
                 in_=grouped[:].rearrange("p w j -> p (w j)"),
             )
 
-        def e2m1_pass(acc, m, a, t0, width, start):
-            h, c0 = divmod(t0, TH)
-            nc.tensor.matmul_mx(
-                out=acc,
-                lhsT=w4[:, a, 2 * P * m : 2 * P * (m + 1)].bitcast(E2M1),
-                lhsT_scale=w4s[:, a, P * m : P * (m + 1)],
-                rhs=x4[h][:, a, 2 * c0 : 2 * (c0 + width)].bitcast(E2M1),
-                rhs_scale=x4s[:, a, t0 : t0 + width],
-                start=start,
-                stop=False,
-            )
+        def regroup_x8(q):
+            return [regroup(raw_x[q], s, nc.vector.tensor_copy, "gx_%d_%d" % (q, s)) for s in range(QUARTER // P)]
 
-        def e4m3_pass(acc, m, t0, width, stop):
-            h, c0 = divmod(t0, TH)
-            nc.tensor.matmul_mx(
-                out=acc,
-                lhsT=w8c[:, P * m : P * (m + 1)].bitcast(E4M3),
-                lhsT_scale=w8s[:, P * m : P * (m + 1)],
-                rhs=x8c[h][:, c0 : c0 + width].bitcast(E4M3),
-                rhs_scale=x8s[h][:, c0 : c0 + width],
-                start=False,
-                stop=stop,
-            )
+        def quantise_x8(q, grouped):
+            h, c0 = divmod(QUARTER * q, HALF)
+            for s in range(QUARTER // P):
+                quantise(grouped[s], x8c[h], x8s[h], c0 // P + s)
 
-        def gelu(dst, acc, m):
-            nc.scalar.activation(out=dst, in_=acc, func=GELU, bias=b_cols[:, 32 * m : 32 * m + 1])
+        def open_bank(q, g):
+            h, c0 = divmod(QUARTER * q, HALF)
+            for i in range(PAIR):
+                m = PAIR * g + i
+                for a in range(PASSES4):
+                    nc.tensor.matmul_mx(
+                        out=banks[q][g][:, i, :],
+                        lhsT=w4[:, a, 2 * P * m : 2 * P * (m + 1)].bitcast(E2M1),
+                        lhsT_scale=w4s[:, a, P * m : P * (m + 1)],
+                        rhs=x4[h][:, a, 2 * c0 : 2 * (c0 + QUARTER)].bitcast(E2M1),
+                        rhs_scale=x4s[:, a, QUARTER * q : QUARTER * (q + 1)],
+                        start=(a == 0 and i == 0),
+                        stop=False,
+                    )
 
-        def store(m0, count, t0, width):
-            h, c0 = divmod(t0, TH)
-            nc.sync.dma_start(
-                out=out_v[:, m0 : m0 + count, t0 : t0 + width], in_=res[h][:, m0 : m0 + count, c0 : c0 + width]
-            )
+        def close_bank(q, g):
+            h, c0 = divmod(QUARTER * q, HALF)
+            cols = slice(c0, c0 + QUARTER)
+            for i in range(PAIR):
+                m = PAIR * g + i
+                nc.tensor.matmul_mx(
+                    out=banks[q][g][:, i, :],
+                    lhsT=w8c[:, P * m : P * (m + 1)].bitcast(E4M3),
+                    lhsT_scale=w8s[:, P * m : P * (m + 1)],
+                    rhs=x8c[h][:, cols].bitcast(E4M3),
+                    rhs_scale=x8s[h][:, cols],
+                    start=False,
+                    stop=(i == PAIR - 1),
+                )
+            for i in range(PAIR):
+                m = PAIR * g + i
+                nc.scalar.activation(
+                    out=res[h][:, m, cols],
+                    in_=banks[q][g][:, i, :],
+                    func=GELU,
+                    bias=b_cols[:, QUAD * m : QUAD * m + 1],
+                )
+            blocks = slice(PAIR * g, PAIR * (g + 1))
+            nc.sync.dma_start(out=out_v[:, blocks, QUARTER * q : QUARTER * (q + 1)], in_=res[h][:, blocks, cols])
 
-        nc.vector.memset(w4s[:].rearrange("p a n -> p (a n)").bitcast(I32), 0)
         nc.vector.memset(x4s[:].rearrange("p a n -> p (a n)").bitcast(I32), 0)
+        nc.vector.memset(w4s[:].rearrange("p a n -> p (a n)").bitcast(I32), 0)
         nc.vector.memset(warm[:], 0.0)
         nc.vector.memset(b_rows[:], 0.0)
         nc.scalar.activation(out=warm_out[:], in_=warm[:], func=GELU)
 
-        nc.sync.dma_start(out=w4[:].bitcast(I32), in_=w4_v.bitcast(I32))
         load_x4(0)
-        load_scales(w4s, w4_scales)
-        load_w8()
+        nc.sync.dma_start(out=w4[:].bitcast(I32), in_=w4_v.bitcast(I32))
         load_scales(x4s, x4_scales)
+        load_w8(0, W8_AHEAD)
+        load_scales(w4s, w4_scales)
+        load_w8(W8_AHEAD, PACK)
         load_bias()
         load_x8(0)
         load_x8(1)
@@ -141,56 +168,35 @@ def tile_mix_atom_fm_gelu_kernel(tc, x8, w8, x4_words, x4_scales, w4_words, w4_s
         load_x8(2)
         load_x8(3)
 
-        for i in range(3):
+        for n in range(WARM_PASSES):
             nc.tensor.matmul_mx(
                 out=banks[3][1][:].rearrange("p i t -> p (i t)"),
-                lhsT=w4[:, 0, 0 : 2 * P].bitcast(E2M1),
-                lhsT_scale=w4s[:, 0, 0:P],
-                rhs=w4[:, 1, :].bitcast(E2M1),
-                rhs_scale=w4s[:, 1, :],
+                lhsT=x4[0][:, 0, 0 : 2 * P].bitcast(E2M1),
+                lhsT_scale=x4s[:, 0, 0:P],
+                rhs=x4[0][:, 1, :].bitcast(E2M1),
+                rhs_scale=x4s[:, 1, 0:HALF],
                 start=True,
                 stop=True,
             )
 
-        def open_bank(q, g):
-            for i in range(2):
-                for a in range(A):
-                    e2m1_pass(banks[q][g][:, i, :], 2 * g + i, a, TQ * q, TQ, a == 0 and i == 0)
-
-        def close_bank(q, g):
-            h, s = divmod(q, 2)
-            for i in range(2):
-                e4m3_pass(banks[q][g][:, i, :], 2 * g + i, TQ * q, TQ, i == 1)
-            for i in range(2):
-                m = 2 * g + i
-                gelu(res[h][:, m, TQ * s : TQ * (s + 1)], banks[q][g][:, i, :], m)
-            store(2 * g, 2, TQ * q, TQ)
-
-        def regroup_x8(q):
-            return [regroup(raw_x[q], i, "vector", "gx_%d_%d" % (q, i)) for i in range(2)]
-
-        def quantise_x8(q, gx):
-            h, s = divmod(q, 2)
-            for i in range(2):
-                quantise(gx[i], x8c[h], x8s[h], 2 * s + i)
-
-        gw = [regroup(raw_w, m, "vector" if m < 2 else "scalar", "gw_%d" % m) for m in range(MT)]
-        quantise(gw[0], w8c, w8s, 0)
-        quantise(gw[1], w8c, w8s, 1)
-        gx = regroup_x8(0)
+        grouped_w = [
+            regroup(raw_w, m, nc.vector.tensor_copy if m < PAIR else nc.scalar.copy, "gw_%d" % m)
+            for m in range(BLOCKS)
+        ]
+        for m in range(PAIR):
+            quantise(grouped_w[m], w8c, w8s, m)
+        grouped_x = regroup_x8(0)
         nc.vector.transpose(out=b_cols[:], in_=b_rows[:])
-        quantise_x8(0, gx)
-        quantise(gw[2], w8c, w8s, 2)
-        quantise(gw[3], w8c, w8s, 3)
+        quantise_x8(0, grouped_x)
+        for m in range(PAIR, BLOCKS):
+            quantise(grouped_w[m], w8c, w8s, m)
 
-        open_bank(0, 0)
-        open_bank(0, 1)
-        open_bank(1, 0)
-        opens_after = (((1, 1), (2, 0)), ((2, 1), (3, 0)), ((3, 1),), ())
-        for q in range(4):
-            if q > 0:
+        opened = 0
+        for n, count in enumerate(OPENS_BEFORE):
+            q, g = divmod(n, PAIR)
+            if q > 0 and g == 0:
                 quantise_x8(q, regroup_x8(q))
-            for g in range(2):
-                close_bank(q, g)
-            for later in opens_after[q]:
-                open_bank(*later)
+            for later in range(opened, opened + count):
+                open_bank(*divmod(later, PAIR))
+            opened = opened + count
+            close_bank(q, g)

@@ -20,9 +20,7 @@ BLOCKS = N_OUT // P
 HALF = T // 2
 QUARTER = T // 4
 PAIR = 2
-W8_AHEAD = 3
 WARM_PASSES = 3
-OPENS_BEFORE = (4, 0, 1, 0, 1, 0, 1, 1)
 
 FLOPS = 2 * (K8 + K4) * N_OUT * T
 
@@ -30,7 +28,7 @@ FLOPS = 2 * (K8 + K4) * N_OUT * T
 def tile_mix_atom_fm_gelu_kernel(tc, x8, w8, x4_words, x4_scales, w4_words, w4_scales, b, out):
     nc = tc.nc
     x8_v = x8.rearrange("(p j) t -> p j t", j=PACK)
-    w8_v = w8.rearrange("(p j) n -> p j n", j=PACK)
+    w8_v = w8.rearrange("(p j) n -> p (j n)", j=PACK)
     x4_v = x4_words.rearrange("a p c -> p a c")
     w4_v = w4_words.rearrange("a p c -> p a c")
     out_v = out.rearrange("(m p) t -> p m t", p=P)
@@ -49,18 +47,17 @@ def tile_mix_atom_fm_gelu_kernel(tc, x8, w8, x4_words, x4_scales, w4_words, w4_s
         x8c = [keep.tile([P, HALF], U32, align_bytes=64, name="x8c_%d" % h) for h in range(2)]
         x8s = [keep.tile([P, HALF], U8, align_bytes=64, name="x8s_%d" % h) for h in range(2)]
         raw_w = keep.tile([P, PACK, N_OUT], F32)
-        raw_x = [keep.tile([P, PACK, QUARTER], F32, name="raw_x_%d" % q) for q in range(4)]
+        raw_first = keep.tile([P, PACK, HALF], F32)
+        raw_x = {q: keep.tile([P, PACK, QUARTER], F32, name="raw_x_%d" % q) for q in (2, 3)}
         res = [keep.tile([P, BLOCKS, HALF], F32, name="res_%d" % h) for h in range(2)]
         b_rows = keep.tile([P, P], F32, align_bytes=64)
         b_cols = keep.tile([P, P], F32, align_bytes=64)
         warm = keep.tile([P, 8], F32)
         warm_out = keep.tile([P, 8], F32)
-        banks = [
-            [psum.tile([P, PAIR, QUARTER], F32, name="bank_%d_%d" % (q, g)) for g in range(PAIR)] for q in range(4)
-        ]
-
-        def load_x8(q):
-            nc.sync.dma_start(out=raw_x[q][:], in_=x8_v[:, :, QUARTER * q : QUARTER * (q + 1)])
+        wide = [psum.tile([P, HALF], F32, name="wide_%d" % m) for m in range(BLOCKS)]
+        banks = {
+            q: [psum.tile([P, PAIR, QUARTER], F32, name="bank_%d_%d" % (q, g)) for g in range(PAIR)] for q in (2, 3)
+        }
 
         def load_x4(h):
             nc.sync.dma_start(
@@ -74,80 +71,70 @@ def tile_mix_atom_fm_gelu_kernel(tc, x8, w8, x4_words, x4_scales, w4_words, w4_s
                     in_=src.rearrange("a (v r) n -> r v a n", r=4)[r].bitcast(I32),
                 )
 
-        def load_w8(j0, j1):
-            nc.sync.dma_start(
-                out=raw_w[:, j0:j1, :].rearrange("p j n -> p (j n)"),
-                in_=w8_v[:, j0:j1, :].rearrange("p j n -> p (j n)"),
-            )
-
-        def load_bias():
-            nc.sync.dma_start(
-                out=b_rows[0:P:QUAD, :].rearrange("v (m i) -> v m i", i=QUAD),
-                in_=b.rearrange("(m v i) -> v m i", v=4, i=QUAD),
-            )
-
-        def regroup(raw, s, copy, name):
-            grouped = keep.tile([P, P, PACK], BF16, align_bytes=64, name=name)
+        def regroup(raw, c0, width, copy, name):
+            grouped = keep.tile([P, width, PACK], BF16, align_bytes=64, name=name)
             copy(
                 out=grouped[:].rearrange("p (c i) j -> p c j i", i=2),
-                in_=raw[:, :, P * s : P * (s + 1)].rearrange("p j (c i) -> p c j i", i=2),
+                in_=raw[:, :, c0 : c0 + width].rearrange("p j (c i) -> p c j i", i=2),
             )
             return grouped
 
-        def quantise(grouped, codes, scales, s):
-            nc.vector.quantize_mx(
-                out=codes[:, P * s : P * (s + 1)].bitcast(E4M3),
-                scales=scales[:, P * s : P * (s + 1)],
-                in_=grouped[:].rearrange("p w j -> p (w j)"),
+        def quantise(grouped, codes, scales):
+            nc.vector.quantize_mx(out=codes.bitcast(E4M3), scales=scales, in_=grouped[:].rearrange("p w j -> p (w j)"))
+
+        def quantise_x8(c0, grouped):
+            h, c = divmod(c0, HALF)
+            quantise(grouped, x8c[h][:, c : c + P], x8s[h][:, c : c + P])
+
+        def pass8(dst, m, c0, width, stop):
+            h, c = divmod(c0, HALF)
+            nc.tensor.matmul_mx(
+                out=dst,
+                lhsT=w8c[:, P * m : P * (m + 1)].bitcast(E4M3),
+                lhsT_scale=w8s[:, P * m : P * (m + 1)],
+                rhs=x8c[h][:, c : c + width].bitcast(E4M3),
+                rhs_scale=x8s[h][:, c : c + width],
+                start=False,
+                stop=stop,
             )
 
-        def regroup_x8(q):
-            return [regroup(raw_x[q], s, nc.vector.tensor_copy, "gx_%d_%d" % (q, s)) for s in range(QUARTER // P)]
+        def pass4(dst, m, a, c0, width, start, stop):
+            h, c = divmod(c0, HALF)
+            nc.tensor.matmul_mx(
+                out=dst,
+                lhsT=w4[:, a, 2 * P * m : 2 * P * (m + 1)].bitcast(E2M1),
+                lhsT_scale=w4s[:, a, P * m : P * (m + 1)],
+                rhs=x4[h][:, a, 2 * c : 2 * (c + width)].bitcast(E2M1),
+                rhs_scale=x4s[:, a, c0 : c0 + width],
+                start=start,
+                stop=stop,
+            )
 
-        def quantise_x8(q, grouped):
-            h, c0 = divmod(QUARTER * q, HALF)
-            for s in range(QUARTER // P):
-                quantise(grouped[s], x8c[h], x8s[h], c0 // P + s)
+        def gelu(dst, src, m):
+            nc.scalar.activation(out=dst, in_=src, func=GELU, bias=b_cols[:, QUAD * m : QUAD * m + 1])
+
+        def open_wide(m):
+            for a in range(PASSES4):
+                pass4(wide[m][:], m, a, 0, HALF, a == 0, False)
+
+        def close_wide(m):
+            pass8(wide[m][:], m, 0, HALF, True)
+            gelu(res[0][:, m, :], wide[m][:], m)
+            nc.sync.dma_start(out=out_v[:, m, 0:HALF], in_=res[0][:, m, :])
 
         def open_bank(q, g):
-            h, c0 = divmod(QUARTER * q, HALF)
             for i in range(PAIR):
-                m = PAIR * g + i
                 for a in range(PASSES4):
-                    nc.tensor.matmul_mx(
-                        out=banks[q][g][:, i, :],
-                        lhsT=w4[:, a, 2 * P * m : 2 * P * (m + 1)].bitcast(E2M1),
-                        lhsT_scale=w4s[:, a, P * m : P * (m + 1)],
-                        rhs=x4[h][:, a, 2 * c0 : 2 * (c0 + QUARTER)].bitcast(E2M1),
-                        rhs_scale=x4s[:, a, QUARTER * q : QUARTER * (q + 1)],
-                        start=(a == 0 and i == 0),
-                        stop=False,
-                    )
+                    pass4(banks[q][g][:, i, :], PAIR * g + i, a, QUARTER * q, QUARTER, a == 0 and i == 0, False)
 
         def close_bank(q, g):
-            h, c0 = divmod(QUARTER * q, HALF)
-            cols = slice(c0, c0 + QUARTER)
+            cols = slice(QUARTER * q - HALF, QUARTER * (q + 1) - HALF)
             for i in range(PAIR):
-                m = PAIR * g + i
-                nc.tensor.matmul_mx(
-                    out=banks[q][g][:, i, :],
-                    lhsT=w8c[:, P * m : P * (m + 1)].bitcast(E4M3),
-                    lhsT_scale=w8s[:, P * m : P * (m + 1)],
-                    rhs=x8c[h][:, cols].bitcast(E4M3),
-                    rhs_scale=x8s[h][:, cols],
-                    start=False,
-                    stop=(i == PAIR - 1),
-                )
+                pass8(banks[q][g][:, i, :], PAIR * g + i, QUARTER * q, QUARTER, i == PAIR - 1)
             for i in range(PAIR):
-                m = PAIR * g + i
-                nc.scalar.activation(
-                    out=res[h][:, m, cols],
-                    in_=banks[q][g][:, i, :],
-                    func=GELU,
-                    bias=b_cols[:, QUAD * m : QUAD * m + 1],
-                )
+                gelu(res[1][:, PAIR * g + i, cols], banks[q][g][:, i, :], PAIR * g + i)
             blocks = slice(PAIR * g, PAIR * (g + 1))
-            nc.sync.dma_start(out=out_v[:, blocks, QUARTER * q : QUARTER * (q + 1)], in_=res[h][:, blocks, cols])
+            nc.sync.dma_start(out=out_v[:, blocks, QUARTER * q : QUARTER * (q + 1)], in_=res[1][:, blocks, cols])
 
         nc.vector.memset(x4s[:].rearrange("p a n -> p (a n)").bitcast(I32), 0)
         nc.vector.memset(w4s[:].rearrange("p a n -> p (a n)").bitcast(I32), 0)
@@ -158,15 +145,16 @@ def tile_mix_atom_fm_gelu_kernel(tc, x8, w8, x4_words, x4_scales, w4_words, w4_s
         load_x4(0)
         nc.sync.dma_start(out=w4[:].bitcast(I32), in_=w4_v.bitcast(I32))
         load_scales(x4s, x4_scales)
-        load_w8(0, W8_AHEAD)
+        nc.sync.dma_start(out=raw_first[:], in_=x8_v[:, :, 0:HALF])
         load_scales(w4s, w4_scales)
-        load_w8(W8_AHEAD, PACK)
-        load_bias()
-        load_x8(0)
-        load_x8(1)
+        nc.sync.dma_start(
+            out=b_rows[0:P:QUAD, :].rearrange("v (m i) -> v m i", i=QUAD),
+            in_=b.rearrange("(m v i) -> v m i", v=4, i=QUAD),
+        )
+        nc.sync.dma_start(out=raw_w[:].rearrange("p j n -> p (j n)"), in_=w8_v)
         load_x4(1)
-        load_x8(2)
-        load_x8(3)
+        for q in (2, 3):
+            nc.sync.dma_start(out=raw_x[q][:], in_=x8_v[:, :, QUARTER * q : QUARTER * (q + 1)])
 
         for n in range(WARM_PASSES):
             nc.tensor.matmul_mx(
@@ -179,24 +167,33 @@ def tile_mix_atom_fm_gelu_kernel(tc, x8, w8, x4_words, x4_scales, w4_words, w4_s
                 stop=True,
             )
 
+        first = [
+            regroup(raw_first, P * s, P, nc.vector.tensor_copy if s < 2 else nc.scalar.copy, "gx_%d" % s)
+            for s in range(HALF // P)
+        ]
+        for s in range(HALF // P):
+            quantise_x8(P * s, first[s])
+        nc.vector.transpose(out=b_cols[:], in_=b_rows[:])
         grouped_w = [
-            regroup(raw_w, m, nc.vector.tensor_copy if m < PAIR else nc.scalar.copy, "gw_%d" % m)
+            regroup(raw_w, P * m, P, nc.vector.tensor_copy if m < 2 else nc.scalar.copy, "gw_%d" % m)
             for m in range(BLOCKS)
         ]
-        for m in range(PAIR):
-            quantise(grouped_w[m], w8c, w8s, m)
-        grouped_x = regroup_x8(0)
-        nc.vector.transpose(out=b_cols[:], in_=b_rows[:])
-        quantise_x8(0, grouped_x)
-        for m in range(PAIR, BLOCKS):
-            quantise(grouped_w[m], w8c, w8s, m)
+        for m in range(BLOCKS):
+            quantise(grouped_w[m], w8c[:, P * m : P * (m + 1)], w8s[:, P * m : P * (m + 1)])
+        for q in (2, 3):
+            grouped = [regroup(raw_x[q], P * s, P, nc.vector.tensor_copy, "gx_%d_%d" % (q, s)) for s in range(2)]
+            for s in range(2):
+                quantise_x8(QUARTER * q + P * s, grouped[s])
 
-        opened = 0
-        for n, count in enumerate(OPENS_BEFORE):
-            q, g = divmod(n, PAIR)
-            if q > 0 and g == 0:
-                quantise_x8(q, regroup_x8(q))
-            for later in range(opened, opened + count):
-                open_bank(*divmod(later, PAIR))
-            opened = opened + count
-            close_bank(q, g)
+        for m in range(BLOCKS):
+            open_wide(m)
+        for g in range(PAIR):
+            for i in range(PAIR):
+                close_wide(PAIR * g + i)
+            open_bank(2, g)
+        for g in range(PAIR):
+            close_bank(2, g)
+        for g in range(PAIR):
+            open_bank(3, g)
+        for g in range(PAIR):
+            close_bank(3, g)

@@ -29,8 +29,6 @@ def tile_mix_atom_fm_gelu_kernel(tc, x8, w8, x4_words, x4_scales, w4_words, w4_s
     nc = tc.nc
     x8_v = x8.rearrange("(p j) t -> p j t", j=PACK)
     w8_v = w8.rearrange("(p j) n -> p (j n)", j=PACK)
-    x4_v = x4_words.rearrange("a p c -> p a c")
-    w4_v = w4_words.rearrange("a p c -> p a c")
     out_v = out.rearrange("(m p) t -> p m t", p=P)
 
     with ExitStack() as ctx:
@@ -38,8 +36,8 @@ def tile_mix_atom_fm_gelu_kernel(tc, x8, w8, x4_words, x4_scales, w4_words, w4_s
         psum = ctx.enter_context(tc.psum_pool(name="psum", bufs=1))
         ctx.enter_context(tc.manual_schedule())
 
-        w4 = keep.tile([P, PASSES4, 2 * N_OUT], U8, align_bytes=64)
-        x4 = [keep.tile([P, PASSES4, 2 * HALF], U8, align_bytes=64, name="x4_%d" % h) for h in range(2)]
+        w4 = [keep.tile([P, 2 * N_OUT], U8, align_bytes=64, name="w4_%d" % a) for a in range(PASSES4)]
+        x4 = [keep.tile([P, 2 * T], U8, align_bytes=64, name="x4_%d" % a) for a in range(PASSES4)]
         w4s = keep.tile([P, PASSES4, N_OUT], U8, align_bytes=64)
         x4s = keep.tile([P, PASSES4, T], U8, align_bytes=64)
         w8c = keep.tile([P, N_OUT], U32, align_bytes=64)
@@ -59,10 +57,9 @@ def tile_mix_atom_fm_gelu_kernel(tc, x8, w8, x4_words, x4_scales, w4_words, w4_s
             q: [psum.tile([P, PAIR, QUARTER], F32, name="bank_%d_%d" % (q, g)) for g in range(PAIR)] for q in (2, 3)
         }
 
-        def load_x4(h):
-            nc.sync.dma_start(
-                out=x4[h][:].bitcast(I32), in_=x4_v[:, :, 2 * HALF * h : 2 * HALF * (h + 1)].bitcast(I32)
-            )
+        def load_words(a):
+            nc.sync.dma_start(out=x4[a][:].bitcast(I32), in_=x4_words[a].bitcast(I32))
+            nc.sync.dma_start(out=w4[a][:].bitcast(I32), in_=w4_words[a].bitcast(I32))
 
         def load_scales(plane, src):
             for r in range(4):
@@ -99,12 +96,11 @@ def tile_mix_atom_fm_gelu_kernel(tc, x8, w8, x4_words, x4_scales, w4_words, w4_s
             )
 
         def pass4(dst, m, a, c0, width, start, stop):
-            h, c = divmod(c0, HALF)
             nc.tensor.matmul_mx(
                 out=dst,
-                lhsT=w4[:, a, 2 * P * m : 2 * P * (m + 1)].bitcast(E2M1),
+                lhsT=w4[a][:, 2 * P * m : 2 * P * (m + 1)].bitcast(E2M1),
                 lhsT_scale=w4s[:, a, P * m : P * (m + 1)],
-                rhs=x4[h][:, a, 2 * c : 2 * (c + width)].bitcast(E2M1),
+                rhs=x4[a][:, 2 * c0 : 2 * (c0 + width)].bitcast(E2M1),
                 rhs_scale=x4s[:, a, c0 : c0 + width],
                 start=start,
                 stop=stop,
@@ -114,27 +110,26 @@ def tile_mix_atom_fm_gelu_kernel(tc, x8, w8, x4_words, x4_scales, w4_words, w4_s
             nc.scalar.activation(out=dst, in_=src, func=GELU, bias=b_cols[:, QUAD * m : QUAD * m + 1])
 
         def open_wide(m):
-            for a in range(PASSES4):
-                pass4(wide[m][:], m, a, 0, HALF, a == 0, False)
+            pass4(wide[m][:], m, 0, 0, HALF, True, False)
 
         def close_wide(m):
+            pass4(wide[m][:], m, 1, 0, HALF, False, False)
             pass8(wide[m][:], m, 0, HALF, True)
             gelu(res[0][:, m, :], wide[m][:], m)
             nc.sync.dma_start(out=out_v[:, m, 0:HALF], in_=res[0][:, m, :])
 
-        def open_bank(q, g):
+        def bank4(q, g, a):
             for i in range(PAIR):
-                for a in range(PASSES4):
-                    pass4(banks[q][g][:, i, :], PAIR * g + i, a, QUARTER * q, QUARTER, a == 0 and i == 0, False)
+                pass4(banks[q][g][:, i, :], PAIR * g + i, a, QUARTER * q, QUARTER, a == 0 and i == 0, False)
 
         def close_bank(q, g):
             cols = slice(QUARTER * q - HALF, QUARTER * (q + 1) - HALF)
             for i in range(PAIR):
                 pass8(banks[q][g][:, i, :], PAIR * g + i, QUARTER * q, QUARTER, i == PAIR - 1)
             for i in range(PAIR):
-                gelu(res[1][:, PAIR * g + i, cols], banks[q][g][:, i, :], PAIR * g + i)
-            blocks = slice(PAIR * g, PAIR * (g + 1))
-            nc.sync.dma_start(out=out_v[:, blocks, QUARTER * q : QUARTER * (q + 1)], in_=res[1][:, blocks, cols])
+                m = PAIR * g + i
+                gelu(res[1][:, m, cols], banks[q][g][:, i, :], m)
+                nc.sync.dma_start(out=out_v[:, m, QUARTER * q : QUARTER * (q + 1)], in_=res[1][:, m, cols])
 
         nc.vector.memset(x4s[:].rearrange("p a n -> p (a n)").bitcast(I32), 0)
         nc.vector.memset(w4s[:].rearrange("p a n -> p (a n)").bitcast(I32), 0)
@@ -142,8 +137,7 @@ def tile_mix_atom_fm_gelu_kernel(tc, x8, w8, x4_words, x4_scales, w4_words, w4_s
         nc.vector.memset(b_rows[:], 0.0)
         nc.scalar.activation(out=warm_out[:], in_=warm[:], func=GELU)
 
-        load_x4(0)
-        nc.sync.dma_start(out=w4[:].bitcast(I32), in_=w4_v.bitcast(I32))
+        load_words(0)
         load_scales(x4s, x4_scales)
         nc.sync.dma_start(out=raw_first[:], in_=x8_v[:, :, 0:HALF])
         load_scales(w4s, w4_scales)
@@ -152,17 +146,17 @@ def tile_mix_atom_fm_gelu_kernel(tc, x8, w8, x4_words, x4_scales, w4_words, w4_s
             in_=b.rearrange("(m v i) -> v m i", v=4, i=QUAD),
         )
         nc.sync.dma_start(out=raw_w[:].rearrange("p j n -> p (j n)"), in_=w8_v)
-        load_x4(1)
+        load_words(1)
         for q in (2, 3):
             nc.sync.dma_start(out=raw_x[q][:], in_=x8_v[:, :, QUARTER * q : QUARTER * (q + 1)])
 
         for n in range(WARM_PASSES):
             nc.tensor.matmul_mx(
                 out=banks[3][1][:].rearrange("p i t -> p (i t)"),
-                lhsT=x4[0][:, 0, 0 : 2 * P].bitcast(E2M1),
+                lhsT=x4[0][:, 0 : 2 * P].bitcast(E2M1),
                 lhsT_scale=x4s[:, 0, 0:P],
-                rhs=x4[0][:, 1, :].bitcast(E2M1),
-                rhs_scale=x4s[:, 1, 0:HALF],
+                rhs=x4[0][:, 2 * HALF : 2 * T].bitcast(E2M1),
+                rhs_scale=x4s[:, 0, HALF:T],
                 start=True,
                 stop=True,
             )
@@ -187,13 +181,15 @@ def tile_mix_atom_fm_gelu_kernel(tc, x8, w8, x4_words, x4_scales, w4_words, w4_s
 
         for m in range(BLOCKS):
             open_wide(m)
+        for q in (2, 3):
+            for g in range(PAIR):
+                bank4(q, g, 0)
+        for m in range(BLOCKS):
+            close_wide(m)
         for g in range(PAIR):
-            for i in range(PAIR):
-                close_wide(PAIR * g + i)
-            open_bank(2, g)
-        for g in range(PAIR):
+            bank4(2, g, 1)
             close_bank(2, g)
         for g in range(PAIR):
-            open_bank(3, g)
+            bank4(3, g, 1)
         for g in range(PAIR):
             close_bank(3, g)

@@ -36,19 +36,19 @@ def tile_mix_atom_fm_gelu_kernel(tc, x8, w8, x4_words, x4_scales, w4_words, w4_s
         psum = ctx.enter_context(tc.psum_pool(name="psum", bufs=1))
         ctx.enter_context(tc.manual_schedule())
 
-        w4 = [keep.tile([P, 2 * N_OUT], U8, align_bytes=64, name="w4_%d" % a) for a in range(PASSES4)]
-        x4 = [keep.tile([P, 2 * T], U8, align_bytes=64, name="x4_%d" % a) for a in range(PASSES4)]
-        w4s = keep.tile([P, PASSES4, N_OUT], U8, align_bytes=64)
-        x4s = keep.tile([P, PASSES4, T], U8, align_bytes=64)
+        w4 = [keep.tile([P, 2 * N_OUT], U8, align_bytes=256, name="w4_%d" % a) for a in range(PASSES4)]
+        x4 = [keep.tile([P, 2 * T], U8, align_bytes=256, name="x4_%d" % a) for a in range(PASSES4)]
+        w4s = keep.tile([P, PASSES4, N_OUT], U8, align_bytes=256)
+        x4s = keep.tile([P, PASSES4, T], U8, align_bytes=256)
         w8c = keep.tile([P, N_OUT], U32, align_bytes=64)
         w8s = keep.tile([P, N_OUT], U8, align_bytes=64)
         x8c = [keep.tile([P, HALF], U32, align_bytes=64, name="x8c_%d" % h) for h in range(2)]
         x8s = [keep.tile([P, HALF], U8, align_bytes=64, name="x8s_%d" % h) for h in range(2)]
-        raw_w = keep.tile([P, PACK, N_OUT], F32)
-        raw_first = keep.tile([P, PACK, HALF], F32)
-        raw_x = {q: keep.tile([P, PACK, QUARTER], F32, name="raw_x_%d" % q) for q in (2, 3)}
-        res = [keep.tile([P, BLOCKS, HALF], F32, name="res_%d" % h) for h in range(2)]
-        b_rows = keep.tile([P, P], F32, align_bytes=64)
+        raw_w = keep.tile([P, PACK, N_OUT], F32, align_bytes=256)
+        raw_first = keep.tile([P, PACK, HALF], F32, align_bytes=256)
+        raw_x = {q: keep.tile([P, PACK, QUARTER], F32, align_bytes=256, name="raw_x_%d" % q) for q in (2, 3)}
+        res = [keep.tile([P, BLOCKS, HALF], F32, align_bytes=256, name="res_%d" % h) for h in range(2)]
+        b_rows = keep.tile([P, P], F32, align_bytes=256)
         b_cols = keep.tile([P, P], F32, align_bytes=64)
         warm = keep.tile([P, 8], F32)
         warm_out = keep.tile([P, 8], F32)

@@ -20,7 +20,7 @@ BLOCKS = N_OUT // P
 HALF = T // 2
 QUARTER = T // 4
 PAIR = 2
-WARM_PASSES = 3
+WARM_WIDTHS = (512, 512, 128)
 
 FLOPS = 2 * (K8 + K4) * N_OUT * T
 
@@ -37,7 +37,8 @@ def tile_mix_atom_fm_gelu_kernel(tc, x8, w8, x4_words, x4_scales, w4_words, w4_s
         ctx.enter_context(tc.manual_schedule())
 
         w4 = [keep.tile([P, 2 * N_OUT], U8, align_bytes=256, name="w4_%d" % a) for a in range(PASSES4)]
-        x4 = [keep.tile([P, 2 * T], U8, align_bytes=256, name="x4_%d" % a) for a in range(PASSES4)]
+        x4_first = keep.tile([P, 2 * T], U8, align_bytes=256)
+        x4_second = [keep.tile([P, 2 * HALF], U8, align_bytes=256, name="x4_second_%d" % h) for h in range(2)]
         w4s = keep.tile([P, PASSES4, N_OUT], U8, align_bytes=256)
         x4s = keep.tile([P, PASSES4, T], U8, align_bytes=256)
         w8c = keep.tile([P, N_OUT], U32, align_bytes=64)
@@ -57,9 +58,14 @@ def tile_mix_atom_fm_gelu_kernel(tc, x8, w8, x4_words, x4_scales, w4_words, w4_s
             q: [psum.tile([P, PAIR, QUARTER], F32, name="bank_%d_%d" % (q, g)) for g in range(PAIR)] for q in (2, 3)
         }
 
-        def load_words(a):
-            nc.sync.dma_start(out=x4[a][:].bitcast(I32), in_=x4_words[a].bitcast(I32))
-            nc.sync.dma_start(out=w4[a][:].bitcast(I32), in_=w4_words[a].bitcast(I32))
+        def load_words(tile, src):
+            nc.sync.dma_start(out=tile[:].bitcast(I32), in_=src.bitcast(I32))
+
+        def x4_cols(a, c0, width):
+            if a == 0:
+                return x4_first[:, 2 * c0 : 2 * (c0 + width)]
+            h, c = divmod(c0, HALF)
+            return x4_second[h][:, 2 * c : 2 * (c + width)]
 
         def load_scales(plane, src):
             for r in range(4):
@@ -74,6 +80,15 @@ def tile_mix_atom_fm_gelu_kernel(tc, x8, w8, x4_words, x4_scales, w4_words, w4_s
                 out=grouped[:].rearrange("p (c i) j -> p c j i", i=2),
                 in_=raw[:, :, c0 : c0 + width].rearrange("p j (c i) -> p c j i", i=2),
             )
+            return grouped
+
+        def regroup_shared(raw, c0, on_vector, name):
+            grouped = keep.tile([P, P, PACK], BF16, align_bytes=64, name=name)
+            for copy, lo, hi in ((nc.vector.tensor_copy, 0, on_vector), (nc.scalar.copy, on_vector, P)):
+                copy(
+                    out=grouped[:, lo:hi, :].rearrange("p (c i) j -> p c j i", i=2),
+                    in_=raw[:, :, c0 + lo : c0 + hi].rearrange("p j (c i) -> p c j i", i=2),
+                )
             return grouped
 
         def quantise(grouped, codes, scales):
@@ -100,7 +115,7 @@ def tile_mix_atom_fm_gelu_kernel(tc, x8, w8, x4_words, x4_scales, w4_words, w4_s
                 out=dst,
                 lhsT=w4[a][:, 2 * P * m : 2 * P * (m + 1)].bitcast(E2M1),
                 lhsT_scale=w4s[:, a, P * m : P * (m + 1)],
-                rhs=x4[a][:, 2 * c0 : 2 * (c0 + width)].bitcast(E2M1),
+                rhs=x4_cols(a, c0, width).bitcast(E2M1),
                 rhs_scale=x4s[:, a, c0 : c0 + width],
                 start=start,
                 stop=stop,
@@ -137,26 +152,30 @@ def tile_mix_atom_fm_gelu_kernel(tc, x8, w8, x4_words, x4_scales, w4_words, w4_s
         nc.vector.memset(b_rows[:], 0.0)
         nc.scalar.activation(out=warm_out[:], in_=warm[:], func=GELU)
 
-        load_words(0)
+        load_words(x4_first, x4_words[0])
+        load_words(w4[0], w4_words[0])
         load_scales(x4s, x4_scales)
-        nc.sync.dma_start(out=raw_first[:], in_=x8_v[:, :, 0:HALF])
+        nc.sync.dma_start(out=raw_first[:, 0:3, :], in_=x8_v[:, 0:3, 0:HALF])
         load_scales(w4s, w4_scales)
+        nc.sync.dma_start(out=raw_first[:, 3:4, :], in_=x8_v[:, 3:4, 0:HALF])
         nc.sync.dma_start(
             out=b_rows[0:P:QUAD, :].rearrange("v (m i) -> v m i", i=QUAD),
             in_=b.rearrange("(m v i) -> v m i", v=4, i=QUAD),
         )
         nc.sync.dma_start(out=raw_w[:].rearrange("p j n -> p (j n)"), in_=w8_v)
-        load_words(1)
-        for q in (2, 3):
-            nc.sync.dma_start(out=raw_x[q][:], in_=x8_v[:, :, QUARTER * q : QUARTER * (q + 1)])
+        load_words(w4[1], w4_words[1])
+        load_words(x4_second[0], x4_words[1][:, 0 : 2 * HALF])
+        nc.sync.dma_start(out=raw_x[2][:], in_=x8_v[:, :, HALF : HALF + QUARTER])
+        load_words(x4_second[1], x4_words[1][:, 2 * HALF : 2 * T])
+        nc.sync.dma_start(out=raw_x[3][:], in_=x8_v[:, :, HALF + QUARTER : T])
 
-        for n in range(WARM_PASSES):
+        for width in WARM_WIDTHS:
             nc.tensor.matmul_mx(
-                out=banks[3][1][:].rearrange("p i t -> p (i t)"),
-                lhsT=x4[0][:, 0 : 2 * P].bitcast(E2M1),
+                out=banks[3][1][:].rearrange("p i t -> p (i t)")[:, 0:width],
+                lhsT=x4_first[:, 0 : 2 * P].bitcast(E2M1),
                 lhsT_scale=x4s[:, 0, 0:P],
-                rhs=x4[0][:, 2 * HALF : 2 * T].bitcast(E2M1),
-                rhs_scale=x4s[:, 0, HALF:T],
+                rhs=x4_first[:, 0 : 2 * width].bitcast(E2M1),
+                rhs_scale=x4s[:, 0, 0:width],
                 start=True,
                 stop=True,
             )
@@ -168,12 +187,18 @@ def tile_mix_atom_fm_gelu_kernel(tc, x8, w8, x4_words, x4_scales, w4_words, w4_s
         for s in range(HALF // P):
             quantise_x8(P * s, first[s])
         nc.vector.transpose(out=b_cols[:], in_=b_rows[:])
-        grouped_w = [
-            regroup(raw_w, P * m, P, nc.vector.tensor_copy if m < 2 else nc.scalar.copy, "gw_%d" % m)
-            for m in range(BLOCKS)
-        ]
-        for m in range(BLOCKS):
-            quantise(grouped_w[m], w8c[:, P * m : P * (m + 1)], w8s[:, P * m : P * (m + 1)])
+
+        def quantise_w8(m, grouped):
+            quantise(grouped, w8c[:, P * m : P * (m + 1)], w8s[:, P * m : P * (m + 1)])
+
+        gw0 = regroup_shared(raw_w, 0, 96, "gw_0")
+        gw1 = regroup_shared(raw_w, P, 64, "gw_1")
+        quantise_w8(0, gw0)
+        gw2 = regroup_shared(raw_w, 2 * P, 64, "gw_2")
+        quantise_w8(1, gw1)
+        gw3 = regroup(raw_w, 3 * P, P, nc.vector.tensor_copy, "gw_3")
+        quantise_w8(2, gw2)
+        quantise_w8(3, gw3)
         for q in (2, 3):
             grouped = [regroup(raw_x[q], P * s, P, nc.vector.tensor_copy, "gx_%d_%d" % (q, s)) for s in range(2)]
             for s in range(2):
@@ -191,5 +216,4 @@ def tile_mix_atom_fm_gelu_kernel(tc, x8, w8, x4_words, x4_scales, w4_words, w4_s
             close_bank(2, g)
         for g in range(PAIR):
             bank4(3, g, 1)
-        for g in range(PAIR):
             close_bank(3, g)

@@ -28,7 +28,7 @@ FLOPS = 2 * (K8 + K4) * N_OUT * T
 def tile_mix_atom_fm_gelu_kernel(tc, x8, w8, x4_words, x4_scales, w4_words, w4_scales, b, out):
     nc = tc.nc
     x8_v = x8.rearrange("(p j) t -> p j t", j=PACK)
-    w8_v = w8.rearrange("(p j) n -> p (j n)", j=PACK)
+    w8_v = w8.rearrange("(p j) n -> p j n", j=PACK)
     out_v = out.rearrange("(m p) t -> p m t", p=P)
 
     with ExitStack() as ctx:
@@ -36,16 +36,19 @@ def tile_mix_atom_fm_gelu_kernel(tc, x8, w8, x4_words, x4_scales, w4_words, w4_s
         psum = ctx.enter_context(tc.psum_pool(name="psum", bufs=1))
         ctx.enter_context(tc.manual_schedule())
 
-        w4 = [keep.tile([P, 2 * N_OUT], U8, align_bytes=256, name="w4_%d" % a) for a in range(PASSES4)]
+        w4_first = keep.tile([P, 2 * N_OUT], U8, align_bytes=256)
+        w4_second = keep.tile([P, 2 * N_OUT], U8, align_bytes=256)
         x4_first = keep.tile([P, 2 * T], U8, align_bytes=256)
-        x4_second = [keep.tile([P, 2 * HALF], U8, align_bytes=256, name="x4_second_%d" % h) for h in range(2)]
+        x4_second = keep.tile([P, 2 * (T - QUARTER)], U8, align_bytes=256)
+        x4_second_tail = keep.tile([P, 2 * QUARTER], U8, align_bytes=256)
         w4s = keep.tile([P, PASSES4, N_OUT], U8, align_bytes=256)
         x4s = keep.tile([P, PASSES4, T], U8, align_bytes=256)
         w8c = keep.tile([P, N_OUT], U32, align_bytes=64)
         w8s = keep.tile([P, N_OUT], U8, align_bytes=64)
         x8c = [keep.tile([P, HALF], U32, align_bytes=64, name="x8c_%d" % h) for h in range(2)]
         x8s = [keep.tile([P, HALF], U8, align_bytes=64, name="x8s_%d" % h) for h in range(2)]
-        raw_w = keep.tile([P, PACK, N_OUT], F32, align_bytes=256)
+        raw_w = keep.tile([P, PACK, N_OUT - P], F32, align_bytes=256)
+        raw_w_last = keep.tile([P, PACK, P], F32, align_bytes=256)
         raw_first = keep.tile([P, PACK, HALF], F32, align_bytes=256)
         raw_x = {q: keep.tile([P, PACK, QUARTER], F32, align_bytes=256, name="raw_x_%d" % q) for q in (2, 3)}
         res = [keep.tile([P, BLOCKS, HALF], F32, align_bytes=256, name="res_%d" % h) for h in range(2)]
@@ -61,11 +64,15 @@ def tile_mix_atom_fm_gelu_kernel(tc, x8, w8, x4_words, x4_scales, w4_words, w4_s
         def load_words(tile, src):
             nc.sync.dma_start(out=tile[:].bitcast(I32), in_=src.bitcast(I32))
 
+        def w4_block(a, m):
+            return (w4_first, w4_second)[a][:, 2 * P * m : 2 * P * (m + 1)]
+
         def x4_cols(a, c0, width):
             if a == 0:
                 return x4_first[:, 2 * c0 : 2 * (c0 + width)]
-            h, c = divmod(c0, HALF)
-            return x4_second[h][:, 2 * c : 2 * (c + width)]
+            if c0 == T - QUARTER:
+                return x4_second_tail[:]
+            return x4_second[:, 2 * c0 : 2 * (c0 + width)]
 
         def load_scales(plane, src):
             for r in range(4):
@@ -113,7 +120,7 @@ def tile_mix_atom_fm_gelu_kernel(tc, x8, w8, x4_words, x4_scales, w4_words, w4_s
         def pass4(dst, m, a, c0, width, start, stop):
             nc.tensor.matmul_mx(
                 out=dst,
-                lhsT=w4[a][:, 2 * P * m : 2 * P * (m + 1)].bitcast(E2M1),
+                lhsT=w4_block(a, m).bitcast(E2M1),
                 lhsT_scale=w4s[:, a, P * m : P * (m + 1)],
                 rhs=x4_cols(a, c0, width).bitcast(E2M1),
                 rhs_scale=x4s[:, a, c0 : c0 + width],
@@ -139,8 +146,11 @@ def tile_mix_atom_fm_gelu_kernel(tc, x8, w8, x4_words, x4_scales, w4_words, w4_s
 
         def close_bank(q, g):
             cols = slice(QUARTER * q - HALF, QUARTER * (q + 1) - HALF)
-            for i in range(PAIR):
-                pass8(banks[q][g][:, i, :], PAIR * g + i, QUARTER * q, QUARTER, i == PAIR - 1)
+            width = P if (q, g) == (3, 0) else QUARTER
+            for c in range(0, QUARTER, width):
+                for i in range(PAIR):
+                    last = i == PAIR - 1 and c + width == QUARTER
+                    pass8(banks[q][g][:, i, c : c + width], PAIR * g + i, QUARTER * q + c, width, last)
             for i in range(PAIR):
                 m = PAIR * g + i
                 gelu(res[1][:, m, cols], banks[q][g][:, i, :], m)
@@ -153,21 +163,22 @@ def tile_mix_atom_fm_gelu_kernel(tc, x8, w8, x4_words, x4_scales, w4_words, w4_s
         nc.scalar.activation(out=warm_out[:], in_=warm[:], func=GELU)
 
         load_words(x4_first, x4_words[0])
-        load_words(w4[0], w4_words[0])
+        load_words(w4_first, w4_words[0])
         load_scales(x4s, x4_scales)
         nc.sync.dma_start(out=raw_first[:, 0:3, :], in_=x8_v[:, 0:3, 0:HALF])
         load_scales(w4s, w4_scales)
         nc.sync.dma_start(out=raw_first[:, 3:4, :], in_=x8_v[:, 3:4, 0:HALF])
+        nc.sync.dma_start(out=raw_w[:], in_=w8_v[:, :, 0 : N_OUT - P])
+        load_words(w4_second, w4_words[1])
+        load_words(x4_second, x4_words[1][:, 0 : 2 * (T - QUARTER)])
         nc.sync.dma_start(
             out=b_rows[0:P:QUAD, :].rearrange("v (m i) -> v m i", i=QUAD),
             in_=b.rearrange("(m v i) -> v m i", v=4, i=QUAD),
         )
-        nc.sync.dma_start(out=raw_w[:].rearrange("p j n -> p (j n)"), in_=w8_v)
-        load_words(w4[1], w4_words[1])
-        load_words(x4_second[0], x4_words[1][:, 0 : 2 * HALF])
+        nc.sync.dma_start(out=raw_w_last[:], in_=w8_v[:, :, N_OUT - P : N_OUT])
         nc.sync.dma_start(out=raw_x[2][:], in_=x8_v[:, :, HALF : HALF + QUARTER])
-        load_words(x4_second[1], x4_words[1][:, 2 * HALF : 2 * T])
         nc.sync.dma_start(out=raw_x[3][:], in_=x8_v[:, :, HALF + QUARTER : T])
+        load_words(x4_second_tail, x4_words[1][:, 2 * (T - QUARTER) : 2 * T])
 
         for width in WARM_WIDTHS:
             nc.tensor.matmul_mx(
@@ -186,7 +197,6 @@ def tile_mix_atom_fm_gelu_kernel(tc, x8, w8, x4_words, x4_scales, w4_words, w4_s
         ]
         for s in range(HALF // P):
             quantise_x8(P * s, first[s])
-        nc.vector.transpose(out=b_cols[:], in_=b_rows[:])
 
         def quantise_w8(m, grouped):
             quantise(grouped, w8c[:, P * m : P * (m + 1)], w8s[:, P * m : P * (m + 1)])
@@ -194,9 +204,10 @@ def tile_mix_atom_fm_gelu_kernel(tc, x8, w8, x4_words, x4_scales, w4_words, w4_s
         gw0 = regroup_shared(raw_w, 0, 96, "gw_0")
         gw1 = regroup_shared(raw_w, P, 64, "gw_1")
         quantise_w8(0, gw0)
-        gw2 = regroup_shared(raw_w, 2 * P, 64, "gw_2")
+        gw2 = regroup_shared(raw_w, 2 * P, 32, "gw_2")
         quantise_w8(1, gw1)
-        gw3 = regroup(raw_w, 3 * P, P, nc.vector.tensor_copy, "gw_3")
+        nc.vector.transpose(out=b_cols[:], in_=b_rows[:])
+        gw3 = regroup(raw_w_last, 0, P, nc.vector.tensor_copy, "gw_3")
         quantise_w8(2, gw2)
         quantise_w8(3, gw3)
         for q in (2, 3):

@@ -14,12 +14,22 @@ GELU = mybir.ActivationFunctionType.Gelu_apprx_tanh
 P = 128
 K8, K4, N_OUT, T = 512, 1024, 512, 1024
 PACK = 4
+FP4_BYTES = 2
 QUAD = 32
+SCALE_ROWS = 4
 PASSES4 = K4 // (P * PACK)
 BLOCKS = N_OUT // P
 HALF = T // 2
 QUARTER = T // 4
-PAIR = 2
+THIRD, FOURTH = 2, 3
+DMA_ALIGN = 256
+MX_ALIGN = 64
+
+ROWS_AHEAD = 3
+W8_CUT = 320
+X8_SHARE = 64
+W8_SHARES = (64, 48)
+W8_LAST_ON_SCALAR = 32
 WARM_WIDTHS = (512, 512, 128)
 
 FLOPS = 2 * (K8 + K4) * N_OUT * T
@@ -30,72 +40,90 @@ def tile_mix_atom_fm_gelu_kernel(tc, x8, w8, x4_words, x4_scales, w4_words, w4_s
     x8_v = x8.rearrange("(p j) t -> p j t", j=PACK)
     w8_v = w8.rearrange("(p j) n -> p j n", j=PACK)
     out_v = out.rearrange("(m p) t -> p m t", p=P)
+    late_quarters = (THIRD, FOURTH)
 
     with ExitStack() as ctx:
         keep = ctx.enter_context(tc.tile_pool(name="keep", bufs=1))
         psum = ctx.enter_context(tc.psum_pool(name="psum", bufs=1))
         ctx.enter_context(tc.manual_schedule())
 
-        w4_first = keep.tile([P, 2 * N_OUT], U8, align_bytes=256)
-        w4_second = keep.tile([P, 2 * N_OUT], U8, align_bytes=256)
-        x4_first = keep.tile([P, 2 * T], U8, align_bytes=256)
-        x4_second = keep.tile([P, 2 * (T - QUARTER)], U8, align_bytes=256)
-        x4_second_tail = keep.tile([P, 2 * QUARTER], U8, align_bytes=256)
-        w4s = keep.tile([P, PASSES4, N_OUT], U8, align_bytes=256)
-        x4s = keep.tile([P, PASSES4, T], U8, align_bytes=256)
-        w8c = keep.tile([P, N_OUT], U32, align_bytes=64)
-        w8s = keep.tile([P, N_OUT], U8, align_bytes=64)
-        x8c = [keep.tile([P, HALF], U32, align_bytes=64, name="x8c_%d" % h) for h in range(2)]
-        x8s = [keep.tile([P, HALF], U8, align_bytes=64, name="x8s_%d" % h) for h in range(2)]
-        raw_w = keep.tile([P, PACK, N_OUT - P], F32, align_bytes=256)
-        raw_w_last = keep.tile([P, PACK, P], F32, align_bytes=256)
-        raw_first = keep.tile([P, PACK, HALF], F32, align_bytes=256)
-        raw_x = {q: keep.tile([P, PACK, QUARTER], F32, align_bytes=256, name="raw_x_%d" % q) for q in (2, 3)}
-        res = [keep.tile([P, BLOCKS, HALF], F32, align_bytes=256, name="res_%d" % h) for h in range(2)]
-        b_rows = keep.tile([P, P], F32, align_bytes=256)
-        b_cols = keep.tile([P, P], F32, align_bytes=64)
+        w4_pass = [keep.tile([P, FP4_BYTES * N_OUT], U8, align_bytes=DMA_ALIGN, name="w4_%d" % a) for a in range(PASSES4)]
+        x4_pass0 = keep.tile([P, FP4_BYTES * T], U8, align_bytes=DMA_ALIGN)
+        x4_pass1_half = keep.tile([P, FP4_BYTES * HALF], U8, align_bytes=DMA_ALIGN)
+        x4_pass1_late = {
+            q: keep.tile([P, FP4_BYTES * QUARTER], U8, align_bytes=DMA_ALIGN, name="x4_late_%d" % q)
+            for q in late_quarters
+        }
+        w4s = keep.tile([P, PASSES4, N_OUT], U8, align_bytes=DMA_ALIGN)
+        x4s = keep.tile([P, PASSES4, T], U8, align_bytes=DMA_ALIGN)
+        w8c = keep.tile([P, N_OUT], U32, align_bytes=MX_ALIGN)
+        w8s = keep.tile([P, N_OUT], U8, align_bytes=MX_ALIGN)
+        x8c = [keep.tile([P, HALF], U32, align_bytes=MX_ALIGN, name="x8c_%d" % h) for h in range(2)]
+        x8s = [keep.tile([P, HALF], U8, align_bytes=MX_ALIGN, name="x8s_%d" % h) for h in range(2)]
+        raw_w_early = keep.tile([P, PACK, W8_CUT], F32, align_bytes=DMA_ALIGN)
+        raw_w_rest = keep.tile([P, PACK, N_OUT - W8_CUT], F32, align_bytes=DMA_ALIGN)
+        raw_half = keep.tile([P, PACK, HALF], F32, align_bytes=DMA_ALIGN)
+        raw_late = {
+            q: keep.tile([P, PACK, QUARTER], F32, align_bytes=DMA_ALIGN, name="raw_late_%d" % q) for q in late_quarters
+        }
+        res = [keep.tile([P, BLOCKS, HALF], F32, align_bytes=DMA_ALIGN, name="res_%d" % h) for h in range(2)]
+        b_rows = keep.tile([P, P], F32, align_bytes=DMA_ALIGN)
+        b_cols = keep.tile([P, P], F32, align_bytes=MX_ALIGN)
         warm = keep.tile([P, 8], F32)
         warm_out = keep.tile([P, 8], F32)
+
         wide = [psum.tile([P, HALF], F32, name="wide_%d" % m) for m in range(BLOCKS)]
-        banks = {
-            q: [psum.tile([P, PAIR, QUARTER], F32, name="bank_%d_%d" % (q, g)) for g in range(PAIR)] for q in (2, 3)
+        spare = [psum.tile([P, HALF], F32, name="spare_%d" % i) for i in range(BLOCKS)]
+        late = {
+            (THIRD, 0): spare[0][:, 0:QUARTER],
+            (THIRD, 1): spare[1][:, 0:QUARTER],
+            (THIRD, 2): spare[2][:, 0:QUARTER],
+            (THIRD, 3): spare[2][:, QUARTER:HALF],
+            (FOURTH, 0): spare[3][:, 0:QUARTER],
+            (FOURTH, 1): wide[0][:, 0:QUARTER],
+            (FOURTH, 2): wide[1][:, 0:QUARTER],
+            (FOURTH, 3): wide[2][:, 0:QUARTER],
         }
+        shared_first, shared_second = (THIRD, 2), (THIRD, 3)
 
         def load_words(tile, src):
             nc.sync.dma_start(out=tile[:].bitcast(I32), in_=src.bitcast(I32))
 
-        def w4_block(a, m):
-            return (w4_first, w4_second)[a][:, 2 * P * m : 2 * P * (m + 1)]
+        def load_scales(plane, src):
+            for r in range(SCALE_ROWS):
+                nc.sync.dma_start(
+                    out=plane[r:P:QUAD, :, :].bitcast(I32),
+                    in_=src.rearrange("a (v r) n -> r v a n", r=SCALE_ROWS)[r].bitcast(I32),
+                )
+
+        def x4_bytes(c0, width):
+            return slice(FP4_BYTES * c0, FP4_BYTES * (c0 + width))
 
         def x4_cols(a, c0, width):
             if a == 0:
-                return x4_first[:, 2 * c0 : 2 * (c0 + width)]
-            if c0 == T - QUARTER:
-                return x4_second_tail[:]
-            return x4_second[:, 2 * c0 : 2 * (c0 + width)]
+                return x4_pass0[:, x4_bytes(c0, width)]
+            if c0 < HALF:
+                return x4_pass1_half[:]
+            return x4_pass1_late[c0 // QUARTER][:]
 
-        def load_scales(plane, src):
-            for r in range(4):
-                nc.sync.dma_start(
-                    out=plane[r:P:QUAD, :, :].bitcast(I32),
-                    in_=src.rearrange("a (v r) n -> r v a n", r=4)[r].bitcast(I32),
-                )
+        def words_tile(name):
+            return keep.tile([P, P, PACK], BF16, align_bytes=MX_ALIGN, name=name)
 
-        def regroup(raw, c0, width, copy, name):
-            grouped = keep.tile([P, width, PACK], BF16, align_bytes=64, name=name)
+        def regroup(copy, grouped, lo, hi, raw, c0):
             copy(
-                out=grouped[:].rearrange("p (c i) j -> p c j i", i=2),
-                in_=raw[:, :, c0 : c0 + width].rearrange("p j (c i) -> p c j i", i=2),
+                out=grouped[:, lo:hi, :].rearrange("p (c i) j -> p c j i", i=2),
+                in_=raw[:, :, c0 : c0 + hi - lo].rearrange("p j (c i) -> p c j i", i=2),
             )
+
+        def regroup_whole(copy, raw, c0, name):
+            grouped = words_tile(name)
+            regroup(copy, grouped, 0, P, raw, c0)
             return grouped
 
         def regroup_shared(raw, c0, on_vector, name):
-            grouped = keep.tile([P, P, PACK], BF16, align_bytes=64, name=name)
-            for copy, lo, hi in ((nc.vector.tensor_copy, 0, on_vector), (nc.scalar.copy, on_vector, P)):
-                copy(
-                    out=grouped[:, lo:hi, :].rearrange("p (c i) j -> p c j i", i=2),
-                    in_=raw[:, :, c0 + lo : c0 + hi].rearrange("p j (c i) -> p c j i", i=2),
-                )
+            grouped = words_tile(name)
+            regroup(nc.vector.tensor_copy, grouped, 0, on_vector, raw, c0)
+            regroup(nc.scalar.copy, grouped, on_vector, P, raw, c0 + on_vector)
             return grouped
 
         def quantise(grouped, codes, scales):
@@ -104,6 +132,9 @@ def tile_mix_atom_fm_gelu_kernel(tc, x8, w8, x4_words, x4_scales, w4_words, w4_s
         def quantise_x8(c0, grouped):
             h, c = divmod(c0, HALF)
             quantise(grouped, x8c[h][:, c : c + P], x8s[h][:, c : c + P])
+
+        def quantise_w8(m, grouped):
+            quantise(grouped, w8c[:, P * m : P * (m + 1)], w8s[:, P * m : P * (m + 1)])
 
         def pass8(dst, m, c0, width, stop):
             h, c = divmod(c0, HALF)
@@ -117,44 +148,43 @@ def tile_mix_atom_fm_gelu_kernel(tc, x8, w8, x4_words, x4_scales, w4_words, w4_s
                 stop=stop,
             )
 
-        def pass4(dst, m, a, c0, width, start, stop):
+        def pass4(dst, m, a, c0, width, start):
             nc.tensor.matmul_mx(
                 out=dst,
-                lhsT=w4_block(a, m).bitcast(E2M1),
+                lhsT=w4_pass[a][:, FP4_BYTES * P * m : FP4_BYTES * P * (m + 1)].bitcast(E2M1),
                 lhsT_scale=w4s[:, a, P * m : P * (m + 1)],
                 rhs=x4_cols(a, c0, width).bitcast(E2M1),
                 rhs_scale=x4s[:, a, c0 : c0 + width],
                 start=start,
-                stop=stop,
+                stop=False,
             )
 
         def gelu(dst, src, m):
             nc.scalar.activation(out=dst, in_=src, func=GELU, bias=b_cols[:, QUAD * m : QUAD * m + 1])
 
-        def open_wide(m):
-            pass4(wide[m][:], m, 0, 0, HALF, True, False)
-
         def close_wide(m):
-            pass4(wide[m][:], m, 1, 0, HALF, False, False)
+            pass4(wide[m][:], m, 1, 0, HALF, False)
             pass8(wide[m][:], m, 0, HALF, True)
             gelu(res[0][:, m, :], wide[m][:], m)
             nc.sync.dma_start(out=out_v[:, m, 0:HALF], in_=res[0][:, m, :])
 
-        def bank4(q, g, a):
-            for i in range(PAIR):
-                pass4(banks[q][g][:, i, :], PAIR * g + i, a, QUARTER * q, QUARTER, a == 0 and i == 0, False)
+        def late4(q, m, a):
+            pass4(late[q, m], m, a, QUARTER * q, QUARTER, a == 0 and (q, m) != shared_second)
 
-        def close_bank(q, g):
-            cols = slice(QUARTER * q - HALF, QUARTER * (q + 1) - HALF)
-            width = P if (q, g) == (3, 0) else QUARTER
+        def late8(q, m):
+            width = P if m == 0 else QUARTER
             for c in range(0, QUARTER, width):
-                for i in range(PAIR):
-                    last = i == PAIR - 1 and c + width == QUARTER
-                    pass8(banks[q][g][:, i, c : c + width], PAIR * g + i, QUARTER * q + c, width, last)
-            for i in range(PAIR):
-                m = PAIR * g + i
-                gelu(res[1][:, m, cols], banks[q][g][:, i, :], m)
-                nc.sync.dma_start(out=out_v[:, m, QUARTER * q : QUARTER * (q + 1)], in_=res[1][:, m, cols])
+                stop = c + width == QUARTER and (q, m) != shared_first
+                pass8(late[q, m][:, c : c + width], m, QUARTER * q + c, width, stop)
+
+        def late_cols(q):
+            return slice(QUARTER * q - HALF, QUARTER * (q + 1) - HALF)
+
+        def late_gelu(q, m):
+            gelu(res[1][:, m, late_cols(q)], late[q, m], m)
+
+        def late_store(q, m0, m1):
+            nc.sync.dma_start(out=out_v[:, m0:m1, QUARTER * q : QUARTER * (q + 1)], in_=res[1][:, m0:m1, late_cols(q)])
 
         nc.vector.memset(x4s[:].rearrange("p a n -> p (a n)").bitcast(I32), 0)
         nc.vector.memset(w4s[:].rearrange("p a n -> p (a n)").bitcast(I32), 0)
@@ -162,69 +192,93 @@ def tile_mix_atom_fm_gelu_kernel(tc, x8, w8, x4_words, x4_scales, w4_words, w4_s
         nc.vector.memset(b_rows[:], 0.0)
         nc.scalar.activation(out=warm_out[:], in_=warm[:], func=GELU)
 
-        load_words(x4_first, x4_words[0])
-        load_words(w4_first, w4_words[0])
+        load_words(x4_pass0, x4_words[0])
+        load_words(w4_pass[0], w4_words[0])
         load_scales(x4s, x4_scales)
-        nc.sync.dma_start(out=raw_first[:, 0:3, :], in_=x8_v[:, 0:3, 0:HALF])
+        nc.sync.dma_start(out=raw_half[:, 0:ROWS_AHEAD, :], in_=x8_v[:, 0:ROWS_AHEAD, 0:HALF])
         load_scales(w4s, w4_scales)
-        nc.sync.dma_start(out=raw_first[:, 3:4, :], in_=x8_v[:, 3:4, 0:HALF])
-        nc.sync.dma_start(out=raw_w[:], in_=w8_v[:, :, 0 : N_OUT - P])
-        load_words(w4_second, w4_words[1])
-        load_words(x4_second, x4_words[1][:, 0 : 2 * (T - QUARTER)])
+        nc.sync.dma_start(out=raw_half[:, ROWS_AHEAD:PACK, :], in_=x8_v[:, ROWS_AHEAD:PACK, 0:HALF])
+        nc.sync.dma_start(out=raw_w_early[:], in_=w8_v[:, :, 0:W8_CUT])
+        load_words(w4_pass[1], w4_words[1])
+        load_words(x4_pass1_half, x4_words[1][:, x4_bytes(0, HALF)])
         nc.sync.dma_start(
             out=b_rows[0:P:QUAD, :].rearrange("v (m i) -> v m i", i=QUAD),
-            in_=b.rearrange("(m v i) -> v m i", v=4, i=QUAD),
+            in_=b.rearrange("(m v i) -> v m i", v=P // QUAD, i=QUAD),
         )
-        nc.sync.dma_start(out=raw_w_last[:], in_=w8_v[:, :, N_OUT - P : N_OUT])
-        nc.sync.dma_start(out=raw_x[2][:], in_=x8_v[:, :, HALF : HALF + QUARTER])
-        nc.sync.dma_start(out=raw_x[3][:], in_=x8_v[:, :, HALF + QUARTER : T])
-        load_words(x4_second_tail, x4_words[1][:, 2 * (T - QUARTER) : 2 * T])
+        nc.sync.dma_start(out=raw_w_rest[:], in_=w8_v[:, :, W8_CUT:N_OUT])
+        for q in late_quarters:
+            nc.sync.dma_start(out=raw_late[q][:], in_=x8_v[:, :, QUARTER * q : QUARTER * (q + 1)])
+            load_words(x4_pass1_late[q], x4_words[1][:, x4_bytes(QUARTER * q, QUARTER)])
 
         for width in WARM_WIDTHS:
             nc.tensor.matmul_mx(
-                out=banks[3][1][:].rearrange("p i t -> p (i t)")[:, 0:width],
-                lhsT=x4_first[:, 0 : 2 * P].bitcast(E2M1),
+                out=spare[3][:, 0:width],
+                lhsT=x4_pass0[:, x4_bytes(0, P)].bitcast(E2M1),
                 lhsT_scale=x4s[:, 0, 0:P],
-                rhs=x4_first[:, 0 : 2 * width].bitcast(E2M1),
+                rhs=x4_pass0[:, x4_bytes(0, width)].bitcast(E2M1),
                 rhs_scale=x4s[:, 0, 0:width],
                 start=True,
                 stop=True,
             )
 
-        first = [
-            regroup(raw_first, P * s, P, nc.vector.tensor_copy if s < 2 else nc.scalar.copy, "gx_%d" % s)
-            for s in range(HALF // P)
-        ]
+        pieces = [regroup_whole(nc.vector.tensor_copy, raw_half, P * s, "gx_%d" % s) for s in range(2)]
+        pieces.append(regroup_shared(raw_half, 2 * P, X8_SHARE, "gx_2"))
+        pieces.append(regroup_whole(nc.scalar.copy, raw_half, 3 * P, "gx_3"))
         for s in range(HALF // P):
-            quantise_x8(P * s, first[s])
+            quantise_x8(P * s, pieces[s])
 
-        def quantise_w8(m, grouped):
-            quantise(grouped, w8c[:, P * m : P * (m + 1)], w8s[:, P * m : P * (m + 1)])
-
-        gw0 = regroup_shared(raw_w, 0, 96, "gw_0")
-        gw1 = regroup_shared(raw_w, P, 64, "gw_1")
+        gw0 = regroup_shared(raw_w_early, 0, W8_SHARES[0], "gw_0")
+        gw1 = regroup_shared(raw_w_early, P, W8_SHARES[1], "gw_1")
         quantise_w8(0, gw0)
-        gw2 = regroup_shared(raw_w, 2 * P, 32, "gw_2")
+        gw2 = words_tile("gw_2")
+        gw3 = words_tile("gw_3")
+        in_early = W8_CUT - 2 * P
+        on_vector = P - W8_LAST_ON_SCALAR
+        regroup(nc.vector.tensor_copy, gw2, 0, in_early, raw_w_early, 2 * P)
         quantise_w8(1, gw1)
         nc.vector.transpose(out=b_cols[:], in_=b_rows[:])
-        gw3 = regroup(raw_w_last, 0, P, nc.vector.tensor_copy, "gw_3")
+        regroup(nc.vector.tensor_copy, gw2, in_early, on_vector, raw_w_rest, 0)
+        regroup(nc.scalar.copy, gw2, on_vector, P, raw_w_rest, on_vector - in_early)
+        regroup(nc.vector.tensor_copy, gw3, 0, P, raw_w_rest, P - in_early)
         quantise_w8(2, gw2)
         quantise_w8(3, gw3)
-        for q in (2, 3):
-            grouped = [regroup(raw_x[q], P * s, P, nc.vector.tensor_copy, "gx_%d_%d" % (q, s)) for s in range(2)]
-            for s in range(2):
-                quantise_x8(QUARTER * q + P * s, grouped[s])
+        for q in late_quarters:
+            pieces = [
+                regroup_whole(nc.vector.tensor_copy, raw_late[q], P * s, "gx_%d_%d" % (q, s))
+                for s in range(QUARTER // P)
+            ]
+            for s in range(QUARTER // P):
+                quantise_x8(QUARTER * q + P * s, pieces[s])
 
         for m in range(BLOCKS):
-            open_wide(m)
-        for q in (2, 3):
-            for g in range(PAIR):
-                bank4(q, g, 0)
+            pass4(wide[m][:], m, 0, 0, HALF, True)
+        for m in range(BLOCKS):
+            late4(THIRD, m, 0)
+        late4(FOURTH, 0, 0)
         for m in range(BLOCKS):
             close_wide(m)
-        for g in range(PAIR):
-            bank4(2, g, 1)
-            close_bank(2, g)
-        for g in range(PAIR):
-            bank4(3, g, 1)
-            close_bank(3, g)
+
+        late4(FOURTH, 1, 0)
+        for m in range(BLOCKS - 1):
+            late4(THIRD, m, 1)
+        for m in (0, 1):
+            late8(THIRD, m)
+            late_gelu(THIRD, m)
+        late_store(THIRD, 0, 2)
+        late4(THIRD, 3, 1)
+        for m in (2, 3):
+            late8(THIRD, m)
+        for m in (2, 3):
+            late_gelu(THIRD, m)
+            late_store(THIRD, m, m + 1)
+
+        late4(FOURTH, 0, 1)
+        late4(FOURTH, 1, 1)
+        late4(FOURTH, 2, 0)
+        passes_left = {0: (), 1: (), 2: (1,), 3: (0, 1)}
+        for m in range(BLOCKS):
+            for a in passes_left[m]:
+                late4(FOURTH, m, a)
+            late8(FOURTH, m)
+            late_gelu(FOURTH, m)
+            late_store(FOURTH, m, m + 1)

@@ -50,10 +50,7 @@ def tile_mix_atom_fm_gelu_kernel(tc, x8, w8, x4_words, x4_scales, w4_words, w4_s
         w4_pass = [keep.tile([P, FP4_BYTES * N_OUT], U8, align_bytes=DMA_ALIGN, name="w4_%d" % a) for a in range(PASSES4)]
         x4_pass0 = keep.tile([P, FP4_BYTES * T], U8, align_bytes=DMA_ALIGN)
         x4_pass1_half = keep.tile([P, FP4_BYTES * HALF], U8, align_bytes=DMA_ALIGN)
-        x4_pass1_late = {
-            q: keep.tile([P, FP4_BYTES * QUARTER], U8, align_bytes=DMA_ALIGN, name="x4_late_%d" % q)
-            for q in late_quarters
-        }
+        x4_pass1_right = keep.tile([P, FP4_BYTES * HALF], U8, align_bytes=DMA_ALIGN)
         w4s = keep.tile([P, PASSES4, N_OUT], U8, align_bytes=DMA_ALIGN)
         x4s = keep.tile([P, PASSES4, T], U8, align_bytes=DMA_ALIGN)
         w8c = keep.tile([P, N_OUT], U32, align_bytes=MX_ALIGN)
@@ -63,8 +60,11 @@ def tile_mix_atom_fm_gelu_kernel(tc, x8, w8, x4_words, x4_scales, w4_words, w4_s
         raw_w_early = keep.tile([P, PACK, W8_CUT], F32, align_bytes=DMA_ALIGN)
         raw_w_rest = keep.tile([P, PACK, N_OUT - W8_CUT], F32, align_bytes=DMA_ALIGN)
         raw_half = keep.tile([P, PACK, HALF], F32, align_bytes=DMA_ALIGN)
+        late_loads = {THIRD: ((0, P), (P, P)), FOURTH: ((0, P), (P, P))}
         raw_late = {
-            q: keep.tile([P, PACK, QUARTER], F32, align_bytes=DMA_ALIGN, name="raw_late_%d" % q) for q in late_quarters
+            (q, c0): keep.tile([P, PACK, width], F32, align_bytes=DMA_ALIGN, name="raw_late_%d_%d" % (q, c0))
+            for q in late_quarters
+            for c0, width in late_loads[q]
         }
         res = [keep.tile([P, BLOCKS, HALF], F32, align_bytes=DMA_ALIGN, name="res_%d" % h) for h in range(2)]
         b_rows = keep.tile([P, P], F32, align_bytes=DMA_ALIGN)
@@ -104,7 +104,7 @@ def tile_mix_atom_fm_gelu_kernel(tc, x8, w8, x4_words, x4_scales, w4_words, w4_s
                 return x4_pass0[:, x4_bytes(c0, width)]
             if c0 < HALF:
                 return x4_pass1_half[:]
-            return x4_pass1_late[c0 // QUARTER][:]
+            return x4_pass1_right[:, x4_bytes(c0 - HALF, width)]
 
         def words_tile(name):
             return keep.tile([P, P, PACK], BF16, align_bytes=MX_ALIGN, name=name)
@@ -207,8 +207,10 @@ def tile_mix_atom_fm_gelu_kernel(tc, x8, w8, x4_words, x4_scales, w4_words, w4_s
         )
         nc.sync.dma_start(out=raw_w_rest[:], in_=w8_v[:, :, W8_CUT:N_OUT])
         for q in late_quarters:
-            nc.sync.dma_start(out=raw_late[q][:], in_=x8_v[:, :, QUARTER * q : QUARTER * (q + 1)])
-            load_words(x4_pass1_late[q], x4_words[1][:, x4_bytes(QUARTER * q, QUARTER)])
+            for c0, width in late_loads[q]:
+                nc.sync.dma_start(out=raw_late[q, c0][:], in_=x8_v[:, :, QUARTER * q + c0 : QUARTER * q + c0 + width])
+            if q == THIRD:
+                load_words(x4_pass1_right, x4_words[1][:, x4_bytes(HALF, HALF)])
 
         for width in WARM_WIDTHS:
             nc.tensor.matmul_mx(
@@ -244,8 +246,9 @@ def tile_mix_atom_fm_gelu_kernel(tc, x8, w8, x4_words, x4_scales, w4_words, w4_s
         quantise_w8(3, gw3)
         for q in late_quarters:
             pieces = [
-                regroup_whole(nc.vector.tensor_copy, raw_late[q], P * s, "gx_%d_%d" % (q, s))
-                for s in range(QUARTER // P)
+                regroup_whole(nc.vector.tensor_copy, raw_late[q, c0], c, "gx_%d_%d" % (q, c0 + c))
+                for c0, width in late_loads[q]
+                for c in range(0, width, P)
             ]
             for s in range(QUARTER // P):
                 quantise_x8(QUARTER * q + P * s, pieces[s])
@@ -258,21 +261,22 @@ def tile_mix_atom_fm_gelu_kernel(tc, x8, w8, x4_words, x4_scales, w4_words, w4_s
         for m in range(BLOCKS):
             close_wide(m)
 
-        late4(FOURTH, 1, 0)
-        for m in range(BLOCKS - 1):
+        for m in (0, 1):
             late4(THIRD, m, 1)
         for m in (0, 1):
             late8(THIRD, m)
             late_gelu(THIRD, m)
         late_store(THIRD, 0, 2)
-        late4(THIRD, 3, 1)
+        for m in (2, 3):
+            late4(THIRD, m, 1)
         for m in (2, 3):
             late8(THIRD, m)
         for m in (2, 3):
             late_gelu(THIRD, m)
-            late_store(THIRD, m, m + 1)
+        late_store(THIRD, 2, 4)
 
         late4(FOURTH, 0, 1)
+        late4(FOURTH, 1, 0)
         late4(FOURTH, 1, 1)
         late4(FOURTH, 2, 0)
         passes_left = {0: (), 1: (), 2: (1,), 3: (0, 1)}

@@ -111,8 +111,8 @@ def tile_mix_atom_fm_gelu_kernel(tc, x8, w8, x4_words, x4_scales, w4_words, w4_s
 
         def regroup(copy, grouped, lo, hi, raw, c0):
             copy(
-                out=grouped[:, lo:hi, :].rearrange("p (c i) j -> p c j i", i=2),
-                in_=raw[:, :, c0 : c0 + hi - lo].rearrange("p j (c i) -> p c j i", i=2),
+                out=grouped[:, lo:hi, :].rearrange("p (c i) j -> p c j i", i=4),
+                in_=raw[:, :, c0 : c0 + hi - lo].rearrange("p j (c i) -> p c j i", i=4),
             )
 
         def regroup_whole(copy, raw, c0, name):

from contextlib import ExitStack

import concourse.mybir as mybir

F32 = mybir.dt.float32
BF16 = mybir.dt.bfloat16
I32 = mybir.dt.int32
U32 = mybir.dt.uint32
U8 = mybir.dt.uint8
E4M3 = mybir.dt.float8_e4m3fn_x4
E2M1 = mybir.dt.float4_e2m1fn_x4
GELU = mybir.ActivationFunctionType.Gelu_apprx_tanh

P = 128
K8, K4, N_OUT, T = 512, 1024, 512, 1024
PACK = 4
FP4_BYTES = 2
QUAD = 32
SCALE_ROWS = 4
PASSES4 = K4 // (P * PACK)
BLOCKS = N_OUT // P
HALF = T // 2
QUARTER = T // 4
THIRD, FOURTH = 2, 3
DMA_ALIGN = 256
MX_ALIGN = 64

ROWS_AHEAD = 3
W8_CUT = 320
X8_SHARE = 64
W8_SHARES = (64, 48)
W8_LAST_ON_SCALAR = 32
WARM_WIDTHS = (512, 512, 128)

FLOPS = 2 * (K8 + K4) * N_OUT * T


def tile_mix_atom_fm_gelu_kernel(tc, x8, w8, x4_words, x4_scales, w4_words, w4_scales, b, out):
    nc = tc.nc
    x8_v = x8.rearrange("(p j) t -> p j t", j=PACK)
    w8_v = w8.rearrange("(p j) n -> p j n", j=PACK)
    out_v = out.rearrange("(m p) t -> p m t", p=P)
    late_quarters = (THIRD, FOURTH)

    with ExitStack() as ctx:
        keep = ctx.enter_context(tc.tile_pool(name="keep", bufs=1))
        psum = ctx.enter_context(tc.psum_pool(name="psum", bufs=1))
        ctx.enter_context(tc.manual_schedule())

        w4_pass = [keep.tile([P, FP4_BYTES * N_OUT], U8, align_bytes=DMA_ALIGN, name="w4_%d" % a) for a in range(PASSES4)]
        x4_pass0 = keep.tile([P, FP4_BYTES * T], U8, align_bytes=DMA_ALIGN)
        x4_pass1_half = keep.tile([P, FP4_BYTES * HALF], U8, align_bytes=DMA_ALIGN)
        x4_pass1_right = keep.tile([P, FP4_BYTES * HALF], U8, align_bytes=DMA_ALIGN)
        w4s = keep.tile([P, PASSES4, N_OUT], U8, align_bytes=DMA_ALIGN)
        x4s = keep.tile([P, PASSES4, T], U8, align_bytes=DMA_ALIGN)
        w8c = keep.tile([P, N_OUT], U32, align_bytes=MX_ALIGN)
        w8s = keep.tile([P, N_OUT], U8, align_bytes=MX_ALIGN)
        x8c = [keep.tile([P, HALF], U32, align_bytes=MX_ALIGN, name="x8c_%d" % h) for h in range(2)]
        x8s = [keep.tile([P, HALF], U8, align_bytes=MX_ALIGN, name="x8s_%d" % h) for h in range(2)]
        raw_w_early = keep.tile([P, PACK, W8_CUT], F32, align_bytes=DMA_ALIGN)
        raw_w_rest = keep.tile([P, PACK, N_OUT - W8_CUT], F32, align_bytes=DMA_ALIGN)
        raw_half = keep.tile([P, PACK, HALF], F32, align_bytes=DMA_ALIGN)
        late_loads = {THIRD: ((0, P), (P, P)), FOURTH: ((0, P), (P, P))}
        raw_late = {
            (q, c0): keep.tile([P, PACK, width], F32, align_bytes=DMA_ALIGN, name="raw_late_%d_%d" % (q, c0))
            for q in late_quarters
            for c0, width in late_loads[q]
        }
        res = [keep.tile([P, BLOCKS, HALF], F32, align_bytes=DMA_ALIGN, name="res_%d" % h) for h in range(2)]
        b_rows = keep.tile([P, P], F32, align_bytes=DMA_ALIGN)
        b_cols = keep.tile([P, P], F32, align_bytes=MX_ALIGN)
        warm = keep.tile([P, 8], F32)
        warm_out = keep.tile([P, 8], F32)

        wide = [psum.tile([P, HALF], F32, name="wide_%d" % m) for m in range(BLOCKS)]
        spare = [psum.tile([P, HALF], F32, name="spare_%d" % i) for i in range(BLOCKS)]
        late = {
            (THIRD, 0): spare[0][:, 0:QUARTER],
            (THIRD, 1): spare[1][:, 0:QUARTER],
            (THIRD, 2): spare[2][:, 0:QUARTER],
            (THIRD, 3): spare[2][:, QUARTER:HALF],
            (FOURTH, 0): spare[3][:, 0:QUARTER],
            (FOURTH, 1): wide[0][:, 0:QUARTER],
            (FOURTH, 2): wide[1][:, 0:QUARTER],
            (FOURTH, 3): wide[2][:, 0:QUARTER],
        }
        shared_first, shared_second = (THIRD, 2), (THIRD, 3)

        def load_words(tile, src):
            nc.sync.dma_start(out=tile[:].bitcast(I32), in_=src.bitcast(I32))

        def load_scales(plane, src):
            for r in range(SCALE_ROWS):
                nc.sync.dma_start(
                    out=plane[r:P:QUAD, :, :].bitcast(I32),
                    in_=src.rearrange("a (v r) n -> r v a n", r=SCALE_ROWS)[r].bitcast(I32),
                )

        def x4_bytes(c0, width):
            return slice(FP4_BYTES * c0, FP4_BYTES * (c0 + width))

        def x4_cols(a, c0, width):
            if a == 0:
                return x4_pass0[:, x4_bytes(c0, width)]
            if c0 < HALF:
                return x4_pass1_half[:]
            return x4_pass1_right[:, x4_bytes(c0 - HALF, width)]

        def words_tile(name):
            return keep.tile([P, P, PACK], BF16, align_bytes=MX_ALIGN, name=name)

        def regroup(copy, grouped, lo, hi, raw, c0):
            copy(
                out=grouped[:, lo:hi, :].rearrange("p (c i) j -> p c j i", i=4),
                in_=raw[:, :, c0 : c0 + hi - lo].rearrange("p j (c i) -> p c j i", i=4),
            )

        def regroup_whole(copy, raw, c0, name):
            grouped = words_tile(name)
            regroup(copy, grouped, 0, P, raw, c0)
            return grouped

        def regroup_shared(raw, c0, on_vector, name):
            grouped = words_tile(name)
            regroup(nc.vector.tensor_copy, grouped, 0, on_vector, raw, c0)
            regroup(nc.scalar.copy, grouped, on_vector, P, raw, c0 + on_vector)
            return grouped

        def quantise(grouped, codes, scales):
            nc.vector.quantize_mx(out=codes.bitcast(E4M3), scales=scales, in_=grouped[:].rearrange("p w j -> p (w j)"))

        def quantise_x8(c0, grouped):
            h, c = divmod(c0, HALF)
            quantise(grouped, x8c[h][:, c : c + P], x8s[h][:, c : c + P])

        def quantise_w8(m, grouped):
            quantise(grouped, w8c[:, P * m : P * (m + 1)], w8s[:, P * m : P * (m + 1)])

        def pass8(dst, m, c0, width, stop):
            h, c = divmod(c0, HALF)
            nc.tensor.matmul_mx(
                out=dst,
                lhsT=w8c[:, P * m : P * (m + 1)].bitcast(E4M3),
                lhsT_scale=w8s[:, P * m : P * (m + 1)],
                rhs=x8c[h][:, c : c + width].bitcast(E4M3),
                rhs_scale=x8s[h][:, c : c + width],
                start=False,
                stop=stop,
            )

        def pass4(dst, m, a, c0, width, start):
            nc.tensor.matmul_mx(
                out=dst,
                lhsT=w4_pass[a][:, FP4_BYTES * P * m : FP4_BYTES * P * (m + 1)].bitcast(E2M1),
                lhsT_scale=w4s[:, a, P * m : P * (m + 1)],
                rhs=x4_cols(a, c0, width).bitcast(E2M1),
                rhs_scale=x4s[:, a, c0 : c0 + width],
                start=start,
                stop=False,
            )

        def gelu(dst, src, m):
            nc.scalar.activation(out=dst, in_=src, func=GELU, bias=b_cols[:, QUAD * m : QUAD * m + 1])

        def close_wide(m):
            pass4(wide[m][:], m, 1, 0, HALF, False)
            pass8(wide[m][:], m, 0, HALF, True)
            gelu(res[0][:, m, :], wide[m][:], m)
            nc.sync.dma_start(out=out_v[:, m, 0:HALF], in_=res[0][:, m, :])

        def late4(q, m, a):
            pass4(late[q, m], m, a, QUARTER * q, QUARTER, a == 0 and (q, m) != shared_second)

        def late8(q, m):
            width = P if m == 0 else QUARTER
            for c in range(0, QUARTER, width):
                stop = c + width == QUARTER and (q, m) != shared_first
                pass8(late[q, m][:, c : c + width], m, QUARTER * q + c, width, stop)

        def late_cols(q):
            return slice(QUARTER * q - HALF, QUARTER * (q + 1) - HALF)

        def late_gelu(q, m):
            gelu(res[1][:, m, late_cols(q)], late[q, m], m)

        def late_store(q, m0, m1):
            nc.sync.dma_start(out=out_v[:, m0:m1, QUARTER * q : QUARTER * (q + 1)], in_=res[1][:, m0:m1, late_cols(q)])

        nc.vector.memset(x4s[:].rearrange("p a n -> p (a n)").bitcast(I32), 0)
        nc.vector.memset(w4s[:].rearrange("p a n -> p (a n)").bitcast(I32), 0)
        nc.vector.memset(warm[:], 0.0)
        nc.vector.memset(b_rows[:], 0.0)
        nc.scalar.activation(out=warm_out[:], in_=warm[:], func=GELU)

        load_words(x4_pass0, x4_words[0])
        load_words(w4_pass[0], w4_words[0])
        load_scales(x4s, x4_scales)
        nc.sync.dma_start(out=raw_half[:, 0:ROWS_AHEAD, :], in_=x8_v[:, 0:ROWS_AHEAD, 0:HALF])
        load_scales(w4s, w4_scales)
        nc.sync.dma_start(out=raw_half[:, ROWS_AHEAD:PACK, :], in_=x8_v[:, ROWS_AHEAD:PACK, 0:HALF])
        nc.sync.dma_start(out=raw_w_early[:], in_=w8_v[:, :, 0:W8_CUT])
        load_words(w4_pass[1], w4_words[1])
        load_words(x4_pass1_half, x4_words[1][:, x4_bytes(0, HALF)])
        nc.sync.dma_start(
            out=b_rows[0:P:QUAD, :].rearrange("v (m i) -> v m i", i=QUAD),
            in_=b.rearrange("(m v i) -> v m i", v=P // QUAD, i=QUAD),
        )
        nc.sync.dma_start(out=raw_w_rest[:], in_=w8_v[:, :, W8_CUT:N_OUT])
        for q in late_quarters:
            for c0, width in late_loads[q]:
                nc.sync.dma_start(out=raw_late[q, c0][:], in_=x8_v[:, :, QUARTER * q + c0 : QUARTER * q + c0 + width])
            if q == THIRD:
                load_words(x4_pass1_right, x4_words[1][:, x4_bytes(HALF, HALF)])

        for width in WARM_WIDTHS:
            nc.tensor.matmul_mx(
                out=spare[3][:, 0:width],
                lhsT=x4_pass0[:, x4_bytes(0, P)].bitcast(E2M1),
                lhsT_scale=x4s[:, 0, 0:P],
                rhs=x4_pass0[:, x4_bytes(0, width)].bitcast(E2M1),
                rhs_scale=x4s[:, 0, 0:width],
                start=True,
                stop=True,
            )

        pieces = [regroup_whole(nc.vector.tensor_copy, raw_half, P * s, "gx_%d" % s) for s in range(2)]
        pieces.append(regroup_shared(raw_half, 2 * P, X8_SHARE, "gx_2"))
        pieces.append(regroup_whole(nc.scalar.copy, raw_half, 3 * P, "gx_3"))
        for s in range(HALF // P):
            quantise_x8(P * s, pieces[s])

        gw0 = regroup_shared(raw_w_early, 0, W8_SHARES[0], "gw_0")
        gw1 = regroup_shared(raw_w_early, P, W8_SHARES[1], "gw_1")
        quantise_w8(0, gw0)
        gw2 = words_tile("gw_2")
        gw3 = words_tile("gw_3")
        in_early = W8_CUT - 2 * P
        on_vector = P - W8_LAST_ON_SCALAR
        regroup(nc.vector.tensor_copy, gw2, 0, in_early, raw_w_early, 2 * P)
        quantise_w8(1, gw1)
        nc.vector.transpose(out=b_cols[:], in_=b_rows[:])
        regroup(nc.vector.tensor_copy, gw2, in_early, on_vector, raw_w_rest, 0)
        regroup(nc.scalar.copy, gw2, on_vector, P, raw_w_rest, on_vector - in_early)
        regroup(nc.vector.tensor_copy, gw3, 0, P, raw_w_rest, P - in_early)
        quantise_w8(2, gw2)
        quantise_w8(3, gw3)
        for q in late_quarters:
            pieces = [
                regroup_whole(nc.vector.tensor_copy, raw_late[q, c0], c, "gx_%d_%d" % (q, c0 + c))
                for c0, width in late_loads[q]
                for c in range(0, width, P)
            ]
            for s in range(QUARTER // P):
                quantise_x8(QUARTER * q + P * s, pieces[s])

        for m in range(BLOCKS):
            pass4(wide[m][:], m, 0, 0, HALF, True)
        for m in range(BLOCKS):
            late4(THIRD, m, 0)
        late4(FOURTH, 0, 0)
        for m in range(BLOCKS):
            close_wide(m)

        for m in (0, 1):
            late4(THIRD, m, 1)
        for m in (0, 1):
            late8(THIRD, m)
            late_gelu(THIRD, m)
        late_store(THIRD, 0, 2)
        for m in (2, 3):
            late4(THIRD, m, 1)
        for m in (2, 3):
            late8(THIRD, m)
        for m in (2, 3):
            late_gelu(THIRD, m)
        late_store(THIRD, 2, 4)

        late4(FOURTH, 0, 1)
        late4(FOURTH, 1, 0)
        late4(FOURTH, 1, 1)
        late4(FOURTH, 2, 0)
        passes_left = {0: (), 1: (), 2: (1,), 3: (0, 1)}
        for m in range(BLOCKS):
            for a in passes_left[m]:
                late4(FOURTH, m, a)
            late8(FOURTH, m)
            late_gelu(FOURTH, m)
            late_store(FOURTH, m, m + 1)
